import numpy as np
import ml_dtypes


def mxq(x, axis, fmt="e4m3"):
    dtype, down = {"e4m3": (ml_dtypes.float8_e4m3fn, 7), "e5m2": (ml_dtypes.float8_e5m2, 14)}[fmt]
    v = np.moveaxis(np.asarray(x, np.float32).astype(ml_dtypes.bfloat16).astype(np.float64), axis, -1)
    blocks = v.reshape(v.shape[:-1] + (-1, 32))
    amax = np.abs(blocks).max(-1, keepdims=True)
    byte = np.maximum(np.where(amax > 0, np.frexp(amax)[1] - 1 + 127, 0) - down, 1)
    scale = np.exp2(byte - 127.0)
    codes = (blocks / scale).astype(np.float32).astype(dtype).astype(np.float64)
    return np.moveaxis((codes * scale).reshape(v.shape), -1, axis)


WIDE = False


def mx_kscale(k):
    if not WIDE:
        return np.ones(k)
    levels = np.array([24, -24, 12, -12, 0])
    if k % 512:
        return np.exp2(np.random.permutation(np.resize(levels, k // 32))).repeat(32)
    a = np.empty((k // 512, 16))
    for p in range(k // 512):
        a[p, :8] = np.random.permutation(np.resize(levels, 8))
        for g in range(8):
            far = levels[np.abs(levels - a[p, g]) >= 10]
            a[p, g + 8] = far[np.random.randint(len(far))]
    return np.exp2(a.ravel()).repeat(32)


def f64(x):
    return np.asarray(x).astype(np.float64)


def striped(idx):
    return np.tile(idx.reshape(-1, 16).T, (8, 1)).astype(np.uint16)


def unstriped(offs):
    return offs[:16].T.reshape(-1).astype(np.int64)


E2M1 = np.array([0.0, 0.5, 1.0, 1.5, 2.0, 3.0, 4.0, 6.0, -0.0, -0.5, -1.0, -1.5, -2.0, -3.0, -4.0, -6.0])


def pack_weight(w, fmt):
    k, n = w.shape
    w = f64(np.asarray(w, np.float32).astype(ml_dtypes.bfloat16)).reshape(k // 32, 32, n)
    amax = np.abs(w).max(1)
    if fmt == "e4m3":
        byte = np.frexp(amax)[1] - 1 + 127 - 7
    else:
        mant, ex = np.frexp(amax / 6.0)
        byte = np.where(mant > 0.5, ex, ex - 1) + 127
    byte = np.clip(np.where(amax > 0, byte, 1), 1, 254)
    scaled = (w * np.exp2(127.0 - byte)[:, None, :]).reshape(k, n).astype(np.float32)
    by_word = np.ascontiguousarray(scaled.reshape(k // 512, 128, 4, n).transpose(0, 1, 3, 2))
    if fmt == "e4m3":
        words = by_word.astype(ml_dtypes.float8_e4m3fn).view(np.uint8)
    else:
        c = by_word.astype(ml_dtypes.float4_e2m1fn).view(np.uint8) & 0xF
        words = (c[..., 0::2] | (c[..., 1::2] << 4)).reshape(k // 512, 128, 2 * n)
    return np.ascontiguousarray(words), np.ascontiguousarray(byte.astype(np.uint8).reshape(k // 512, 16, n))


def unpack_weight(words, scales, fmt):
    g, _, n = scales.shape
    words = np.ascontiguousarray(words).reshape(g, 128, n, -1)
    if fmt == "e4m3":
        vals = words.view(ml_dtypes.float8_e4m3fn).astype(np.float64)
    else:
        nib = np.empty((g, 128, n, 4), np.uint8)
        nib[..., 0::2] = words & 0xF
        nib[..., 1::2] = words >> 4
        vals = E2M1[nib]
    vals = vals * np.repeat(np.exp2(scales.astype(np.float64) - 127.0), 8, axis=1)[..., None]
    return vals.transpose(0, 1, 3, 2).reshape(g * 512, n)


def planes(y):
    n, m = y.shape
    v = y.astype(np.float32).astype(ml_dtypes.bfloat16).astype(np.float64).reshape(n // 32, 32, m)
    top = np.abs(v).max(1)
    byte = np.clip(np.where(top > 0, np.frexp(top)[1] - 1 + 127 - 7, 1), 1, 254)
    codes = (v * np.exp2(127.0 - byte)[:, None, :]).reshape(n, m).astype(np.float32).astype(ml_dtypes.float8_e4m3fn).view(np.uint8)
    words = codes.reshape(n // 512, 128, 4, m).transpose(0, 1, 3, 2)
    return np.ascontiguousarray(words), np.ascontiguousarray(byte.astype(np.uint8).reshape(n // 512, 16, m))


def sigm(f):
    return 1.0 / (1.0 + np.exp(-np.maximum(f, -700.0)))


K, N, T, J = 1024, 512, 2048, 1024


def setup_inputs():
    n = np.random.standard_normal
    s = mx_kscale(K)[:, None]
    p_tab = pack_weight(n((K, T)) * s, "e4m3")
    p_wa = pack_weight(n((K, N)) / np.sqrt(2 * K) / s, "e2m1")
    p_wb = pack_weight(n((K, N)) / np.sqrt(2 * K) / s, "e2m1")
    p_wo = pack_weight(n((K, N)) / np.sqrt(K) / s, "e2m1")
    return {
        "tab_words": p_tab[0],
        "tab_scales": p_tab[1],
        "wa_words": p_wa[0],
        "wa_scales": p_wa[1],
        "wb_words": p_wb[0],
        "wb_scales": p_wb[1],
        "wc": (n((K, N)) / np.sqrt(K) / s).astype(np.float32),
        "wo_words": p_wo[0],
        "wo_scales": p_wo[1],
        "rT": (n((N, T))).astype(np.float32),
        "wgo": np.tile(np.random.uniform(0.5, 2.0, J), (128, 1)).astype(np.float32),
        "offs": striped(np.random.permutation(T)[:J]),
        "offs2": striped(np.random.permutation(T)[:J]),
    }


def reference(tab_words, tab_scales, wa_words, wa_scales, wb_words, wb_scales, wc, wo_words, wo_scales, rT, wgo, offs, offs2):
    idx = unstriped(offs)
    idx2 = unstriped(offs2)
    tab_ = unpack_weight(tab_words, tab_scales, "e4m3")[:, idx]
    tabb_ = unpack_weight(tab_words, tab_scales, "e4m3")[:, idx2]
    wa_ = unpack_weight(wa_words, wa_scales, "e2m1")
    wb_ = unpack_weight(wb_words, wb_scales, "e2m1")
    za = wa_.T @ tabb_ + wb_.T @ tab_
    eta = sigm(za)
    wc_ = mxq(f64(wc), 0, "e4m3")
    ms = wc_.T @ tab_
    wo_ = unpack_weight(wo_words, wo_scales, "e2m1")
    ow = wo_.T @ tabb_
    out = np.zeros((N, T))
    out[:, idx2] = f64(wgo)[0] * (ow + eta * ms + f64(rT)[:, idx2])
    return (out,) + planes(out)

@@ -1,0 +1,269 @@
+from contextlib import ExitStack
+
+import concourse.mybir as mybir
+from concourse.masks import make_identity
+
+K, N, T, J = 1024, 512, 2048, 1024
+FLOPS = 4 * 2 * K * N * J
+
+F32 = mybir.dt.float32
+BF16 = mybir.dt.bfloat16
+I32 = mybir.dt.int32
+U32 = mybir.dt.uint32
+U16 = mybir.dt.uint16
+U8 = mybir.dt.uint8
+FP8X4 = mybir.dt.float8_e4m3fn_x4
+FP4X4 = mybir.dt.float4_e2m1fn_x4
+MULT = mybir.AluOpType.mult
+ADD = mybir.AluOpType.add
+SIGMOID = mybir.ActivationFunctionType.Sigmoid
+
+P = 128
+PACK = 4
+PASSES = 2
+HALF = J // 2
+QUARTER = J // 4
+CHUNK = 512
+
+
+def tile_list_rgg_ownLP_kernel(
+    tc, tab_words, tab_scales, wa_words, wa_scales, wb_words, wb_scales, wc, wo_words, wo_scales,
+    rT, wgo, offs, offs2, out_0, out_1, out_2,
+):
+    nc = tc.nc
+    with ExitStack() as ctx:
+        lists = ctx.enter_context(tc.tile_pool(name="lists", bufs=1))
+        keep = ctx.enter_context(tc.tile_pool(name="keep", bufs=1))
+        psum = ctx.enter_context(tc.psum_pool(name="psum", bufs=2))
+
+        src_list = lists.tile([P, J // 16], U16, name="src_list")
+        dst_list = lists.tile([P, J // 16], U16, name="dst_list")
+        edge_lists = (dst_list, src_list)
+
+        def offsets(lst, j0, j1):
+            return lst[:, j0 // 16 : j1 // 16]
+
+        tab_planes = keep.tile([P, T], U8, name="tab_planes", align_bytes=64)
+        nc.vector.memset(tab_planes[:].bitcast(I32), 0)
+        w_planes = keep.tile([P, 3, PASSES, N], U8, name="w_planes", align_bytes=64)
+        nc.vector.memset(w_planes[:].rearrange("p w a n -> p (w a n)").bitcast(I32), 0)
+        moved = [[keep.tile([P, HALF], U8, name="moved%d%d" % (e, h,), align_bytes=64) for h in range(2)] for e in range(2)]
+        for e in range(2):
+            for h in range(2):
+                nc.vector.memset(moved[e][h][:].bitcast(I32), 0)
+        pages = [keep.tile([P, T], F32, name="page%d" % (t,)) for t in range(2)]
+        for t in range(2):
+            nc.vector.memset(pages[t][:].bitcast(I32), 0)
+        ident = keep.tile([P, P], F32, name="ident")
+        make_identity(nc, ident[:])
+
+        table = [keep.tile([P, T], I32, name="table%d" % (a,), tag="late%d" % (a,), align_bytes=64) for a in range(PASSES)]
+
+        def load_table(a):
+            nc.sync.dma_start(table[a][:], tab_words[a].rearrange("p t i -> p (t i)").bitcast(I32))
+
+        nc.sync.dma_start(dst_list[:], offs2)
+        landed = [keep.tile([P, T // 4], I32, name="landed%d" % (u,), tag="page_late%d" % (u,)) for u in range(2)]
+        for q in range(4):
+            nc.sync.dma_start(landed[q % 2][32 * q : 32 * q + 8, :], tab_scales[:, 4 * q : 4 * q + 4, :].bitcast(I32))
+        load_table(0)
+        for q in range(4):
+            nc.vector.tensor_copy(tab_planes[32 * q : 32 * q + 8, :].bitcast(I32), landed[q % 2][32 * q : 32 * q + 8, :])
+        for u in range(2):
+            pages.append(keep.tile([P, T], F32, name="page%d" % (2 + u,), tag="page_late%d" % (u,)))
+            nc.gpsimd.memset(pages[2 + u][:].bitcast(I32), 0)
+        w_rows = keep.tile([16, 3, PASSES, N // 4], I32, name="w_rows")
+        for w, src in enumerate((wa_scales, wb_scales, wo_scales)):
+            nc.sync.dma_start(w_rows[:, w, :, :], src.rearrange("a q n -> q a n").bitcast(I32))
+        nc.sync.dma_start(src_list[:], offs)
+        load_table(1)
+
+        wc_raw = [keep.tile([P, PACK, N], F32, name="wc_raw%d" % (a,), tag="early%d" % (a,), align_bytes=64) for a in range(PASSES)]
+
+        def load_wc(a):
+            nc.sync.dma_start(wc_raw[a][:], wc[512 * a : 512 * (a + 1), :].rearrange("(p i) n -> p i n", i=PACK))
+
+        load_wc(0)
+        load_wc(1)
+        w_words = []
+        for w, src in enumerate((wa_words, wb_words, wo_words)):
+            tile_w = keep.tile([P, PASSES, 2 * N], U8, name="w_words%d" % (w,), align_bytes=64)
+            nc.sync.dma_start(tile_w[:].bitcast(I32), src.rearrange("a p b -> p a b").bitcast(I32))
+            w_words.append(tile_w)
+        for q in range(4):
+            nc.scalar.dma_start(
+                w_planes[32 * q : 32 * q + 4].rearrange("p w a n -> p (w a n)").bitcast(I32),
+                w_rows[4 * q : 4 * q + 4].rearrange("p w a n -> p (w a n)"),
+            )
+        r_rows = rT.rearrange("(p i) t -> p i t", i=PACK)
+        state = {}
+
+        def load_state(t, tag, align):
+            state[t] = keep.tile([P, T], F32, name="state%d" % (t,), tag=tag, align_bytes=align)
+            nc.sync.dma_start(state[t][:], r_rows[:, t, :])
+
+        picked_planes = [[None, None], [None, None]]
+
+        def gather_planes(e, h):
+            g = keep.tile([P, HALF], U8, name="picked_planes%d%d" % (e, h,), align_bytes=64)
+            nc.vector.tensor_copy(g[:], tab_planes[:].indirect(offsets(edge_lists[e], h * HALF, (h + 1) * HALF)))
+            nc.gpsimd.dma_start(moved[e][h][0:100, :].bitcast(I32), g[4:104, :].bitcast(I32))
+            picked_planes[e][h] = g
+
+        def gather_words(dst, e, a, j0, j1):
+            nc.vector.tensor_copy(dst, table[a][:].bitcast(U32).indirect(offsets(edge_lists[e], j0, j1)))
+
+        first = keep.tile([P, 2, PASSES, HALF], U32, name="first", align_bytes=64)
+        gather_words(first[:, 0, 0, :], 0, 0, 0, HALF)
+        gather_planes(0, 0)
+        gather_planes(1, 0)
+        gather_words(first[:, 1, 0, :], 1, 0, 0, HALF)
+        gather_words(first[:, 0, 1, :], 0, 1, 0, HALF)
+        gather_words(first[:, 1, 1, :], 1, 1, 0, HALF)
+        gather_planes(0, 1)
+        gather_planes(1, 1)
+
+        wc_codes = keep.tile([P, PASSES, N], U32, name="wc_codes", align_bytes=64)
+        wc_planes = keep.tile([P, PASSES, N], U8, name="wc_planes", align_bytes=64)
+        for a in range(PASSES):
+            grouped = keep.tile([P, N, PACK], BF16, name="grouped%d" % (a,), tag="hold_a%d" % (a,), align_bytes=64)
+            nc.scalar.copy(
+                grouped[:].rearrange("p (c u) i -> p c i u", u=4),
+                wc_raw[a][:].rearrange("p i (c u) -> p c i u", u=4),
+            )
+            nc.vector.quantize_mx(
+                out=wc_codes[:, a, :].bitcast(FP8X4),
+                scales=wc_planes[:, a, :],
+                in_=grouped[:].rearrange("p n i -> p (n i)"),
+            )
+            load_state(a, "early%d" % (a,), 64)
+        weight = keep.tile([P, J], F32, name="weight", tag="hold_a0", align_bytes=64)
+        nc.sync.dma_start(weight[:], wgo)
+
+        def gather_quarter(q, tag):
+            g = keep.tile([P, 2, PASSES, QUARTER], U32, name="later%d" % (q,), tag=tag, align_bytes=64)
+            for a in range(PASSES):
+                for e in range(2):
+                    gather_words(g[:, e, a, :], e, a, q * QUARTER, (q + 1) * QUARTER)
+            return g
+
+        later = {2: gather_quarter(2, "hold_a1")}
+
+        def picked(b, e, a):
+            h, c = divmod(b * P, HALF)
+            plane = (picked_planes if a == 0 else moved)[e][h][:, c : c + P]
+            if h == 0:
+                words = first[:, e, a, c : c + P]
+            else:
+                q, cq = divmod(b * P, QUARTER)
+                words = later[q][:, e, a, cq : cq + P]
+            return words.bitcast(FP8X4), plane
+
+        def dealt(bank):
+            return bank[:].rearrange("j (m t) -> j t m", t=PACK)
+
+        message = {}
+        own = {}
+
+        def products(b):
+            def group(bank, terms):
+                for i, (e, a, rhs, rhs_plane) in enumerate(terms):
+                    words, plane = picked(b, e, a)
+                    nc.tensor.matmul_mx(out=bank[:], lhsT=words, lhsT_scale=plane, rhs=rhs, rhs_scale=rhs_plane,
+                                        start=(i == 0), stop=(i == len(terms) - 1))
+
+            def fp4(w, a):
+                return w_words[w][:, a, :].bitcast(FP4X4), w_planes[:, w, a, :]
+
+            za = psum.tile([P, N], F32, name="za")
+            group(za, [(e, a) + fp4(e, a) for a in range(PASSES) for e in range(2)])
+            ow = psum.tile([P, N], F32, name="ow")
+            group(ow, [(0, a) + fp4(2, a) for a in range(PASSES)])
+            ms = psum.tile([P, N], F32, name="ms")
+            group(ms, [(1, a, wc_codes[:, a, :].bitcast(FP8X4), wc_planes[:, a, :]) for a in range(PASSES)])
+            if b == 1:
+                eta = keep.tile([P, PACK, P], F32, name="eta_hold", tag="hold_b", align_bytes=64)
+            else:
+                eta = keep.tile([P, PACK, P], F32, name="eta", bufs=2)
+            nc.scalar.activation(eta[:], dealt(za), SIGMOID)
+            own[b] = keep.tile([P, PACK, P], F32, name="own%d" % (b,))
+            nc.scalar.copy(own[b][:], dealt(ow))
+            message[b] = keep.tile([P, PACK, P], F32, name="message%d" % (b,))
+            nc.vector.tensor_tensor(message[b][:], dealt(ms), eta[:], MULT)
+
+        def turn(dst, parts):
+            bank = psum.tile([P, 4, P], F32, name="turned")
+            for s, (t, b) in enumerate(parts):
+                nc.tensor.matmul(bank[:, s, :], own[b][:, t, :], ident[:], start=True, stop=False, is_transpose=True)
+                nc.tensor.matmul(bank[:, s, :], message[b][:, t, :], ident[:], start=False, stop=True, is_transpose=True)
+            nc.scalar.copy(dst, bank[:].rearrange("p s j -> p (s j)"))
+
+        def add_state(t, j0, j1, summed, name):
+            total = keep.tile([P, j1 - j0], F32, name=name)
+            nc.vector.tensor_tensor(total[:], state[t][:].indirect(offsets(dst_list, j0, j1)), summed, ADD)
+            return total
+
+        def scatter(t, j0, j1, total):
+            nc.vector.tensor_tensor(pages[t][:].indirect(offsets(dst_list, j0, j1)), total[:], weight[:, j0:j1], MULT)
+
+        def early_pages(q):
+            summed = keep.tile([P, 2 * QUARTER], F32, name="summed", bufs=2)
+            turn(summed[:], [(t, b) for t in range(2) for b in (2 * q, 2 * q + 1)])
+            j0, j1 = q * QUARTER, (q + 1) * QUARTER
+            totals = [add_state(t, j0, j1, summed[:, t * QUARTER : (t + 1) * QUARTER], "total%d%d" % (t, q % 2,)) for t in range(2)]
+            for t in range(2):
+                scatter(t, j0, j1, totals[t])
+
+        products(0)
+        products(1)
+        later[3] = gather_quarter(3, "hold_b")
+        load_state(2, "late0", 64)
+        load_state(3, "late1", 64)
+        products(2)
+        products(3)
+        early_pages(0)
+        products(4)
+        products(5)
+        early_pages(1)
+        products(6)
+        products(7)
+        early_pages(2)
+        early_pages(3)
+        for t in (2, 3):
+            summed = keep.tile([P, J], F32, name="summed_all%d" % (t,))
+            for h in range(2):
+                turn(summed[:, h * HALF : (h + 1) * HALF], [(t, b) for b in range(4 * h, 4 * h + 4)])
+            scatter(t, 0, J, add_state(t, 0, J, summed[:], "total_all"))
+
+        out_rows = out_0.rearrange("(p i) t -> p i t", i=PACK)
+        for t in range(PACK):
+            nc.sync.dma_start(out_rows[:, t, :], pages[t][:])
+
+        woven = [keep.tile([P, CHUNK, PACK], BF16, name="woven%d" % (c,), align_bytes=64) for c in range(4)]
+        for t in range(3):
+            for c in range(4):
+                cols = slice(c * CHUNK, (c + 1) * CHUNK)
+                if t == 2 and c < 2:
+                    nc.scalar.copy(woven[c][:, :, 2:4], pages[t][:, cols].unsqueeze(2).to_broadcast([P, CHUNK, 2]))
+                else:
+                    nc.scalar.copy(woven[c][:, :, t], pages[t][:, cols])
+        for c in range(4):
+            cols = slice(c * CHUNK, (c + 1) * CHUNK)
+            if c < 2:
+                nc.vector.tensor_copy(woven[c][:, :, 3], pages[3][:, cols])
+            else:
+                nc.scalar.copy(woven[c][:, :, 3], pages[3][:, cols])
+        out_plane = keep.tile([P, T], U8, name="out_plane", align_bytes=64)
+        out_words = out_1[0].rearrange("p t i -> p (t i)").bitcast(I32)
+        for c in range(4):
+            cols = slice(c * CHUNK, (c + 1) * CHUNK)
+            codes = keep.tile([P, CHUNK], U32, name="codes%d" % (c,), align_bytes=64)
+            nc.vector.quantize_mx(
+                out=codes[:].bitcast(FP8X4),
+                scales=out_plane[:, cols],
+                in_=woven[c][:].rearrange("p c i -> p (c i)"),
+            )
+            nc.sync.dma_start(out_words[:, cols], codes[:].bitcast(I32))
+        for q in range(4):
+            eng = nc.sync if q % 2 == 0 else nc.scalar
+            eng.dma_start(out_2[0, 4 * q : 4 * q + 4, :].bitcast(I32), out_plane[32 * q : 32 * q + 4, :].bitcast(I32))

@@ -47,43 +47,45 @@ def tile_list_rgg_ownLP_kernel(
         nc.vector.memset(tab_planes[:].bitcast(I32), 0)
         w_planes = keep.tile([P, 3, PASSES, N], U8, name="w_planes", align_bytes=64)
         nc.vector.memset(w_planes[:].rearrange("p w a n -> p (w a n)").bitcast(I32), 0)
-        moved = [[keep.tile([P, HALF], U8, name="moved%d%d" % (e, h,), align_bytes=64) for h in range(2)] for e in range(2)]
-        for e in range(2):
-            for h in range(2):
-                nc.vector.memset(moved[e][h][:].bitcast(I32), 0)
-        pages = [keep.tile([P, T], F32, name="page%d" % (t,)) for t in range(2)]
-        for t in range(2):
-            nc.vector.memset(pages[t][:].bitcast(I32), 0)
+        moved_all = keep.tile([P, 4 * HALF], U8, name="moved_all", align_bytes=64)
+        nc.vector.memset(moved_all[:].bitcast(I32), 0)
+        moved = [[moved_all[:, (2 * e + h) * HALF : (2 * e + h + 1) * HALF] for h in range(2)] for e in range(2)]
+        pages = [keep.tile([P, T], F32, name="page0")]
+        nc.vector.memset(pages[0][:].bitcast(I32), 0)
+
+        def late_page(tag):
+            page = keep.tile([P, T], F32, name="page%d" % (len(pages),), tag=tag, align_bytes=64)
+            nc.gpsimd.memset(page[:].bitcast(I32), 0)
+            pages.append(page)
+
         ident = keep.tile([P, P], F32, name="ident")
         make_identity(nc, ident[:])
+        warm = keep.tile([P, 1], F32, name="warm")
+        nc.scalar.activation(warm[:], ident[:, 0:1], SIGMOID)
 
         table = [keep.tile([P, T], I32, name="table%d" % (a,), tag="late%d" % (a,), align_bytes=64) for a in range(PASSES)]
 
         def load_table(a):
             nc.sync.dma_start(table[a][:], tab_words[a].rearrange("p t i -> p (t i)").bitcast(I32))
 
-        nc.sync.dma_start(dst_list[:], offs2)
-        landed = [keep.tile([P, T // 4], I32, name="landed%d" % (u,), tag="page_late%d" % (u,)) for u in range(2)]
-        for q in range(4):
-            nc.sync.dma_start(landed[q % 2][32 * q : 32 * q + 8, :], tab_scales[:, 4 * q : 4 * q + 4, :].bitcast(I32))
-        load_table(0)
-        for q in range(4):
-            nc.vector.tensor_copy(tab_planes[32 * q : 32 * q + 8, :].bitcast(I32), landed[q % 2][32 * q : 32 * q + 8, :])
-        for u in range(2):
-            pages.append(keep.tile([P, T], F32, name="page%d" % (2 + u,), tag="page_late%d" % (u,)))
-            nc.gpsimd.memset(pages[2 + u][:].bitcast(I32), 0)
-        w_rows = keep.tile([16, 3, PASSES, N // 4], I32, name="w_rows")
-        for w, src in enumerate((wa_scales, wb_scales, wo_scales)):
-            nc.sync.dma_start(w_rows[:, w, :, :], src.rearrange("a q n -> q a n").bitcast(I32))
-        nc.sync.dma_start(src_list[:], offs)
-        load_table(1)
-
         wc_raw = [keep.tile([P, PACK, N], F32, name="wc_raw%d" % (a,), tag="early%d" % (a,), align_bytes=64) for a in range(PASSES)]
 
         def load_wc(a):
             nc.sync.dma_start(wc_raw[a][:], wc[512 * a : 512 * (a + 1), :].rearrange("(p i) n -> p i n", i=PACK))
 
+        nc.sync.dma_start(dst_list[:], offs2)
+        nc.sync.dma_start(src_list[:], offs)
+        landed = keep.tile([P, T // 4], I32, name="landed", tag="page1", align_bytes=64)
+        for q in range(4):
+            nc.sync.dma_start(landed[32 * q : 32 * q + 8, :], tab_scales[:, 4 * q : 4 * q + 4, :].bitcast(I32))
+        load_table(0)
+        for q in range(4):
+            nc.vector.tensor_copy(tab_planes[32 * q : 32 * q + 8, :].bitcast(I32), landed[32 * q : 32 * q + 8, :])
         load_wc(0)
+        w_rows = keep.tile([16, 3, PASSES, N // 4], I32, name="w_rows", tag="weight", align_bytes=64)
+        for w, src in enumerate((wa_scales, wb_scales, wo_scales)):
+            nc.sync.dma_start(w_rows[:, w, :, :], src.rearrange("a q n -> q a n").bitcast(I32))
+        load_table(1)
         load_wc(1)
         w_words = []
         for w, src in enumerate((wa_words, wb_words, wo_words)):
@@ -91,10 +93,13 @@ def tile_list_rgg_ownLP_kernel(
             nc.sync.dma_start(tile_w[:].bitcast(I32), src.rearrange("a p b -> p a b").bitcast(I32))
             w_words.append(tile_w)
         for q in range(4):
-            nc.scalar.dma_start(
+            nc.sync.dma_start(
                 w_planes[32 * q : 32 * q + 4].rearrange("p w a n -> p (w a n)").bitcast(I32),
                 w_rows[4 * q : 4 * q + 4].rearrange("p w a n -> p (w a n)"),
             )
+        late_page("page1")
+        weight = keep.tile([P, J], F32, name="weight", tag="weight", align_bytes=64)
+        nc.sync.dma_start(weight[:], wgo)
         r_rows = rT.rearrange("(p i) t -> p i t", i=PACK)
         state = {}
 
@@ -104,63 +109,57 @@ def tile_list_rgg_ownLP_kernel(
 
         picked_planes = [[None, None], [None, None]]
 
-        def gather_planes(e, h):
-            g = keep.tile([P, HALF], U8, name="picked_planes%d%d" % (e, h,), align_bytes=64)
-            nc.vector.tensor_copy(g[:], tab_planes[:].indirect(offsets(edge_lists[e], h * HALF, (h + 1) * HALF)))
-            nc.gpsimd.dma_start(moved[e][h][0:100, :].bitcast(I32), g[4:104, :].bitcast(I32))
-            picked_planes[e][h] = g
+        def gather_planes(h, tag):
+            g = keep.tile([P, 2, HALF], U8, name="picked_planes%d" % (h,), tag=tag, align_bytes=64)
+            for e in range(2):
+                nc.vector.tensor_copy(g[:, e, :], tab_planes[:].indirect(offsets(edge_lists[e], h * HALF, (h + 1) * HALF)))
+                nc.gpsimd.dma_start(moved[e][h][0:100, :].bitcast(I32), g[4:104, e, :].bitcast(I32))
+                picked_planes[e][h] = g[:, e, :]
 
         def gather_words(dst, e, a, j0, j1):
             nc.vector.tensor_copy(dst, table[a][:].bitcast(U32).indirect(offsets(edge_lists[e], j0, j1)))
 
-        first = keep.tile([P, 2, PASSES, HALF], U32, name="first", align_bytes=64)
+        first = keep.tile([P, 2, PASSES, HALF], U32, name="first", tag="first", align_bytes=64)
+        gather_planes(0, "planes0")
         gather_words(first[:, 0, 0, :], 0, 0, 0, HALF)
-        gather_planes(0, 0)
-        gather_planes(1, 0)
         gather_words(first[:, 1, 0, :], 1, 0, 0, HALF)
         gather_words(first[:, 0, 1, :], 0, 1, 0, HALF)
         gather_words(first[:, 1, 1, :], 1, 1, 0, HALF)
-        gather_planes(0, 1)
-        gather_planes(1, 1)
 
         wc_codes = keep.tile([P, PASSES, N], U32, name="wc_codes", align_bytes=64)
         wc_planes = keep.tile([P, PASSES, N], U8, name="wc_planes", align_bytes=64)
         for a in range(PASSES):
-            grouped = keep.tile([P, N, PACK], BF16, name="grouped%d" % (a,), tag="hold_a%d" % (a,), align_bytes=64)
+            grouped = keep.tile([P, PACK, P, PACK], BF16, name="grouped%d" % (a,), tag="hold_a%d" % (a,), align_bytes=64)
             nc.scalar.copy(
-                grouped[:].rearrange("p (c u) i -> p c i u", u=4),
-                wc_raw[a][:].rearrange("p i (c u) -> p c i u", u=4),
+                grouped[:].rearrange("p t m i -> p m i t"),
+                wc_raw[a][:].rearrange("p i (m t) -> p m i t", t=PACK),
             )
             nc.vector.quantize_mx(
                 out=wc_codes[:, a, :].bitcast(FP8X4),
                 scales=wc_planes[:, a, :],
-                in_=grouped[:].rearrange("p n i -> p (n i)"),
+                in_=grouped[:].rearrange("p t m i -> p (t m i)"),
             )
             load_state(a, "early%d" % (a,), 64)
-        weight = keep.tile([P, J], F32, name="weight", tag="hold_a0", align_bytes=64)
-        nc.sync.dma_start(weight[:], wgo)
+            if a == 0:
+                gather_planes(1, "hold_a0")
 
-        def gather_quarter(q, tag):
-            g = keep.tile([P, 2, PASSES, QUARTER], U32, name="later%d" % (q,), tag=tag, align_bytes=64)
-            for a in range(PASSES):
-                for e in range(2):
-                    gather_words(g[:, e, a, :], e, a, q * QUARTER, (q + 1) * QUARTER)
-            return g
-
-        later = {2: gather_quarter(2, "hold_a1")}
+        second = keep.tile([P, 2, PASSES, HALF], U32, name="second", tag="hold_a1", align_bytes=64)
+        for a in range(PASSES):
+            for e in range(2):
+                gather_words(second[:, e, a, :], e, a, HALF, J)
+            load_state(2 + a, "late%d" % (a,), 64)
 
         def picked(b, e, a):
             h, c = divmod(b * P, HALF)
             plane = (picked_planes if a == 0 else moved)[e][h][:, c : c + P]
-            if h == 0:
-                words = first[:, e, a, c : c + P]
-            else:
-                q, cq = divmod(b * P, QUARTER)
-                words = later[q][:, e, a, cq : cq + P]
+            words = (first, second)[h][:, e, a, c : c + P]
             return words.bitcast(FP8X4), plane
 
-        def dealt(bank):
-            return bank[:].rearrange("j (m t) -> j t m", t=PACK)
+        def dealing(tile):
+            return tile[:].rearrange("j t m -> j m t")
+
+        def by_word(bank):
+            return bank[:].rearrange("j (m t) -> j m t", t=PACK)
 
         message = {}
         own = {}
@@ -177,19 +176,16 @@ def tile_list_rgg_ownLP_kernel(
 
             za = psum.tile([P, N], F32, name="za")
             group(za, [(e, a) + fp4(e, a) for a in range(PASSES) for e in range(2)])
-            ow = psum.tile([P, N], F32, name="ow")
+            ow = psum.tile([P, N], F32, name="ow", bufs=1)
             group(ow, [(0, a) + fp4(2, a) for a in range(PASSES)])
-            ms = psum.tile([P, N], F32, name="ms")
+            ms = psum.tile([P, N], F32, name="ms", bufs=3)
             group(ms, [(1, a, wc_codes[:, a, :].bitcast(FP8X4), wc_planes[:, a, :]) for a in range(PASSES)])
-            if b == 1:
-                eta = keep.tile([P, PACK, P], F32, name="eta_hold", tag="hold_b", align_bytes=64)
-            else:
-                eta = keep.tile([P, PACK, P], F32, name="eta", bufs=2)
-            nc.scalar.activation(eta[:], dealt(za), SIGMOID)
-            own[b] = keep.tile([P, PACK, P], F32, name="own%d" % (b,))
-            nc.scalar.copy(own[b][:], dealt(ow))
+            eta = keep.tile([P, PACK, P], F32, name="eta", bufs=4)
+            nc.scalar.activation(dealing(eta), by_word(za), SIGMOID)
+            own[b] = keep.tile([P, PACK, P], F32, name="own%d" % (b,), tag="own%d" % (b,), align_bytes=64)
+            nc.scalar.copy(dealing(own[b]), by_word(ow))
             message[b] = keep.tile([P, PACK, P], F32, name="message%d" % (b,))
-            nc.vector.tensor_tensor(message[b][:], dealt(ms), eta[:], MULT)
+            nc.vector.tensor_tensor(message[b][:], ms[:].rearrange("j (t m) -> j t m", t=PACK), eta[:], MULT)
 
         def turn(dst, parts):
             bank = psum.tile([P, 4, P], F32, name="turned")
@@ -216,17 +212,16 @@ def tile_list_rgg_ownLP_kernel(
 
         products(0)
         products(1)
-        later[3] = gather_quarter(3, "hold_b")
-        load_state(2, "late0", 64)
-        load_state(3, "late1", 64)
         products(2)
         products(3)
+        late_page("first")
         early_pages(0)
         products(4)
         products(5)
         early_pages(1)
         products(6)
         products(7)
+        late_page("hold_a1")
         early_pages(2)
         early_pages(3)
         for t in (2, 3):
@@ -236,23 +231,29 @@ def tile_list_rgg_ownLP_kernel(
             scatter(t, 0, J, add_state(t, 0, J, summed[:], "total_all"))
 
         out_rows = out_0.rearrange("(p i) t -> p i t", i=PACK)
-        for t in range(PACK):
+        woven = keep.tile([P, T, PACK], BF16, name="woven", align_bytes=64)
+        for c in range(4):
+            cols = slice(c * CHUNK, (c + 1) * CHUNK)
+            pair = keep.tile([P, 2, CHUNK], F32, name="pair%d" % (c,))
+            for t in range(2):
+                nc.sync.dma_start(pair[:, t, :], pages[t][:, cols])
+            if c < 3:
+                nc.scalar.copy(woven[:, cols, 0:2], pair[:].rearrange("p t c -> p c t"))
+            else:
+                nc.scalar.copy(
+                    woven[:, cols, :].rearrange("p c (u t) -> p c u t", u=2),
+                    pair[:].rearrange("p t c -> p c t").unsqueeze(2).to_broadcast([P, CHUNK, 2, 2]),
+                )
+            nc.sync.dma_start(out_rows[:, 0:2, cols], pair[:])
+        for t in (2, 3):
             nc.sync.dma_start(out_rows[:, t, :], pages[t][:])
-
-        woven = [keep.tile([P, CHUNK, PACK], BF16, name="woven%d" % (c,), align_bytes=64) for c in range(4)]
-        for t in range(3):
-            for c in range(4):
-                cols = slice(c * CHUNK, (c + 1) * CHUNK)
-                if t == 2 and c < 2:
-                    nc.scalar.copy(woven[c][:, :, 2:4], pages[t][:, cols].unsqueeze(2).to_broadcast([P, CHUNK, 2]))
-                else:
-                    nc.scalar.copy(woven[c][:, :, t], pages[t][:, cols])
+        nc.scalar.copy(woven[:, :, 2:4], pages[2][:].unsqueeze(2).to_broadcast([P, T, 2]))
         for c in range(4):
             cols = slice(c * CHUNK, (c + 1) * CHUNK)
             if c < 2:
-                nc.vector.tensor_copy(woven[c][:, :, 3], pages[3][:, cols])
+                nc.vector.tensor_copy(woven[:, cols, 3], pages[3][:, cols])
             else:
-                nc.scalar.copy(woven[c][:, :, 3], pages[3][:, cols])
+                nc.scalar.copy(woven[:, cols, 3], pages[3][:, cols])
         out_plane = keep.tile([P, T], U8, name="out_plane", align_bytes=64)
         out_words = out_1[0].rearrange("p t i -> p (t i)").bitcast(I32)
         for c in range(4):
@@ -261,7 +262,7 @@ def tile_list_rgg_ownLP_kernel(
             nc.vector.quantize_mx(
                 out=codes[:].bitcast(FP8X4),
                 scales=out_plane[:, cols],
-                in_=woven[c][:].rearrange("p c i -> p (c i)"),
+                in_=woven[:, cols, :].rearrange("p c i -> p (c i)"),
             )
             nc.sync.dma_start(out_words[:, cols], codes[:].bitcast(I32))
         for q in range(4):

@@ -50,18 +50,11 @@ def tile_list_rgg_ownLP_kernel(
         moved_all = keep.tile([P, 4 * HALF], U8, name="moved_all", align_bytes=64)
         nc.vector.memset(moved_all[:].bitcast(I32), 0)
         moved = [[moved_all[:, (2 * e + h) * HALF : (2 * e + h + 1) * HALF] for h in range(2)] for e in range(2)]
-        pages = [keep.tile([P, T], F32, name="page0")]
-        nc.vector.memset(pages[0][:].bitcast(I32), 0)
-
-        def late_page(tag):
-            page = keep.tile([P, T], F32, name="page%d" % (len(pages),), tag=tag, align_bytes=64)
-            nc.gpsimd.memset(page[:].bitcast(I32), 0)
-            pages.append(page)
-
+        pages = [keep.tile([P, T], F32, name="page%d" % (t,)) for t in range(PACK)]
+        for t in range(PACK):
+            nc.vector.memset(pages[t][:].bitcast(I32), 0)
         ident = keep.tile([P, P], F32, name="ident")
         make_identity(nc, ident[:])
-        warm = keep.tile([P, 1], F32, name="warm")
-        nc.scalar.activation(warm[:], ident[:, 0:1], SIGMOID)
 
         table = [keep.tile([P, T], I32, name="table%d" % (a,), tag="late%d" % (a,), align_bytes=64) for a in range(PASSES)]
 
@@ -75,7 +68,7 @@ def tile_list_rgg_ownLP_kernel(
 
         nc.sync.dma_start(dst_list[:], offs2)
         nc.sync.dma_start(src_list[:], offs)
-        landed = keep.tile([P, T // 4], I32, name="landed", tag="page1", align_bytes=64)
+        landed = keep.tile([P, T // 4], I32, name="landed")
         for q in range(4):
             nc.sync.dma_start(landed[32 * q : 32 * q + 8, :], tab_scales[:, 4 * q : 4 * q + 4, :].bitcast(I32))
         load_table(0)
@@ -97,7 +90,6 @@ def tile_list_rgg_ownLP_kernel(
                 w_planes[32 * q : 32 * q + 4].rearrange("p w a n -> p (w a n)").bitcast(I32),
                 w_rows[4 * q : 4 * q + 4].rearrange("p w a n -> p (w a n)"),
             )
-        late_page("page1")
         weight = keep.tile([P, J], F32, name="weight", tag="weight", align_bytes=64)
         nc.sync.dma_start(weight[:], wgo)
         r_rows = rT.rearrange("(p i) t -> p i t", i=PACK)
@@ -113,13 +105,13 @@ def tile_list_rgg_ownLP_kernel(
             g = keep.tile([P, 2, HALF], U8, name="picked_planes%d" % (h,), tag=tag, align_bytes=64)
             for e in range(2):
                 nc.vector.tensor_copy(g[:, e, :], tab_planes[:].indirect(offsets(edge_lists[e], h * HALF, (h + 1) * HALF)))
-                nc.gpsimd.dma_start(moved[e][h][0:100, :].bitcast(I32), g[4:104, e, :].bitcast(I32))
+                nc.sync.dma_start(moved[e][h][0:100, :].bitcast(I32), g[4:104, e, :].bitcast(I32))
                 picked_planes[e][h] = g[:, e, :]
 
         def gather_words(dst, e, a, j0, j1):
             nc.vector.tensor_copy(dst, table[a][:].bitcast(U32).indirect(offsets(edge_lists[e], j0, j1)))
 
-        first = keep.tile([P, 2, PASSES, HALF], U32, name="first", tag="first", align_bytes=64)
+        first = keep.tile([P, 2, PASSES, HALF], U32, name="first", align_bytes=64)
         gather_planes(0, "planes0")
         gather_words(first[:, 0, 0, :], 0, 0, 0, HALF)
         gather_words(first[:, 1, 0, :], 1, 0, 0, HALF)
@@ -214,14 +206,12 @@ def tile_list_rgg_ownLP_kernel(
         products(1)
         products(2)
         products(3)
-        late_page("first")
         early_pages(0)
         products(4)
         products(5)
         early_pages(1)
         products(6)
         products(7)
-        late_page("hold_a1")
         early_pages(2)
         early_pages(3)
         for t in (2, 3):

@@ -17,6 +17,7 @@ FP4X4 = mybir.dt.float4_e2m1fn_x4
 MULT = mybir.AluOpType.mult
 ADD = mybir.AluOpType.add
 SIGMOID = mybir.ActivationFunctionType.Sigmoid
+COPY = mybir.ActivationFunctionType.Copy
 
 P = 128
 PACK = 4
@@ -24,6 +25,7 @@ PASSES = 2
 HALF = J // 2
 QUARTER = J // 4
 CHUNK = 512
+EDGE = 8
 
 
 def tile_list_rgg_ownLP_kernel(
@@ -44,15 +46,14 @@ def tile_list_rgg_ownLP_kernel(
             return lst[:, j0 // 16 : j1 // 16]
 
         tab_planes = keep.tile([P, T], U8, name="tab_planes", align_bytes=64)
-        nc.vector.memset(tab_planes[:].bitcast(I32), 0)
+        nc.gpsimd.memset(tab_planes[:].bitcast(I32), 0)
         w_planes = keep.tile([P, 3, PASSES, N], U8, name="w_planes", align_bytes=64)
         nc.vector.memset(w_planes[:].rearrange("p w a n -> p (w a n)").bitcast(I32), 0)
-        moved_all = keep.tile([P, 4 * HALF], U8, name="moved_all", align_bytes=64)
-        nc.vector.memset(moved_all[:].bitcast(I32), 0)
-        moved = [[moved_all[:, (2 * e + h) * HALF : (2 * e + h + 1) * HALF] for h in range(2)] for e in range(2)]
-        pages = [keep.tile([P, T], F32, name="page%d" % (t,)) for t in range(PACK)]
-        for t in range(PACK):
-            nc.vector.memset(pages[t][:].bitcast(I32), 0)
+        moved = keep.tile([P, 2, 2, HALF], U8, name="moved", align_bytes=64)
+        nc.vector.memset(moved[:].rearrange("p h e j -> p (h e j)").bitcast(I32), 0)
+        pages = [keep.tile([P, T], F32, name="page%d" % (u,)) for u in range(2)]
+        for u in range(2):
+            nc.vector.memset(pages[u][:].bitcast(I32), 0)
         ident = keep.tile([P, P], F32, name="ident")
         make_identity(nc, ident[:])
 
@@ -68,29 +69,26 @@ def tile_list_rgg_ownLP_kernel(
 
         nc.sync.dma_start(dst_list[:], offs2)
         nc.sync.dma_start(src_list[:], offs)
-        landed = keep.tile([P, T // 4], I32, name="landed")
-        for q in range(4):
-            nc.sync.dma_start(landed[32 * q : 32 * q + 8, :], tab_scales[:, 4 * q : 4 * q + 4, :].bitcast(I32))
-        load_table(0)
-        for q in range(4):
-            nc.vector.tensor_copy(tab_planes[32 * q : 32 * q + 8, :].bitcast(I32), landed[32 * q : 32 * q + 8, :])
-        load_wc(0)
-        w_rows = keep.tile([16, 3, PASSES, N // 4], I32, name="w_rows", tag="weight", align_bytes=64)
+        w_rows = keep.tile([16, 3, PASSES, N // 4], I32, name="w_rows", tag="w_rows", align_bytes=64)
         for w, src in enumerate((wa_scales, wb_scales, wo_scales)):
             nc.sync.dma_start(w_rows[:, w, :, :], src.rearrange("a q n -> q a n").bitcast(I32))
-        load_table(1)
-        load_wc(1)
-        w_words = []
-        for w, src in enumerate((wa_words, wb_words, wo_words)):
-            tile_w = keep.tile([P, PASSES, 2 * N], U8, name="w_words%d" % (w,), align_bytes=64)
-            nc.sync.dma_start(tile_w[:].bitcast(I32), src.rearrange("a p b -> p a b").bitcast(I32))
-            w_words.append(tile_w)
+        for q in range(4):
+            nc.sync.dma_start(tab_planes[32 * q : 32 * q + 8, :].bitcast(I32), tab_scales[:, 4 * q : 4 * q + 4, :].bitcast(I32))
+        load_table(0)
         for q in range(4):
             nc.sync.dma_start(
                 w_planes[32 * q : 32 * q + 4].rearrange("p w a n -> p (w a n)").bitcast(I32),
                 w_rows[4 * q : 4 * q + 4].rearrange("p w a n -> p (w a n)"),
             )
-        weight = keep.tile([P, J], F32, name="weight", tag="weight", align_bytes=64)
+        load_wc(0)
+        load_wc(1)
+        load_table(1)
+        w_words = []
+        for w, src in enumerate((wa_words, wb_words, wo_words)):
+            tile_w = keep.tile([P, PASSES, 2 * N], U8, name="w_words%d" % (w,), align_bytes=64)
+            nc.sync.dma_start(tile_w[:].bitcast(I32), src.rearrange("a p b -> p a b").bitcast(I32))
+            w_words.append(tile_w)
+        weight = keep.tile([P, J], F32, name="weight", align_bytes=64)
         nc.sync.dma_start(weight[:], wgo)
         r_rows = rT.rearrange("(p i) t -> p i t", i=PACK)
         state = {}
@@ -99,20 +97,26 @@ def tile_list_rgg_ownLP_kernel(
             state[t] = keep.tile([P, T], F32, name="state%d" % (t,), tag=tag, align_bytes=align)
             nc.sync.dma_start(state[t][:], r_rows[:, t, :])
 
-        picked_planes = [[None, None], [None, None]]
+        load_state(0, "w_rows", 64)
 
-        def gather_planes(h, tag):
-            g = keep.tile([P, 2, HALF], U8, name="picked_planes%d" % (h,), tag=tag, align_bytes=64)
+        picked_planes = {}
+
+        def gather_planes(h):
+            g = keep.tile([P, 2, HALF], U8, name="picked_planes%d" % (h,), align_bytes=64)
             for e in range(2):
                 nc.vector.tensor_copy(g[:, e, :], tab_planes[:].indirect(offsets(edge_lists[e], h * HALF, (h + 1) * HALF)))
-                nc.sync.dma_start(moved[e][h][0:100, :].bitcast(I32), g[4:104, e, :].bitcast(I32))
-                picked_planes[e][h] = g[:, e, :]
+            nc.sync.dma_start(
+                moved[0:100, h].rearrange("p e j -> p (e j)").bitcast(I32),
+                g[4:104].rearrange("p e j -> p (e j)").bitcast(I32),
+            )
+            picked_planes[h] = g
 
         def gather_words(dst, e, a, j0, j1):
             nc.vector.tensor_copy(dst, table[a][:].bitcast(U32).indirect(offsets(edge_lists[e], j0, j1)))
 
         first = keep.tile([P, 2, PASSES, HALF], U32, name="first", align_bytes=64)
-        gather_planes(0, "planes0")
+        gather_planes(0)
+        gather_planes(1)
         gather_words(first[:, 0, 0, :], 0, 0, 0, HALF)
         gather_words(first[:, 1, 0, :], 1, 0, 0, HALF)
         gather_words(first[:, 0, 1, :], 0, 1, 0, HALF)
@@ -131,19 +135,18 @@ def tile_list_rgg_ownLP_kernel(
                 scales=wc_planes[:, a, :],
                 in_=grouped[:].rearrange("p t m i -> p (t m i)"),
             )
-            load_state(a, "early%d" % (a,), 64)
-            if a == 0:
-                gather_planes(1, "hold_a0")
+            load_state(1 + a, "early%d" % (a,), 64)
 
         second = keep.tile([P, 2, PASSES, HALF], U32, name="second", tag="hold_a1", align_bytes=64)
         for a in range(PASSES):
             for e in range(2):
                 gather_words(second[:, e, a, :], e, a, HALF, J)
-            load_state(2 + a, "late%d" % (a,), 64)
+        load_state(3, "late1", 64)
+
 
         def picked(b, e, a):
             h, c = divmod(b * P, HALF)
-            plane = (picked_planes if a == 0 else moved)[e][h][:, c : c + P]
+            plane = picked_planes[h][:, e, c : c + P] if a == 0 else moved[:, h, e, c : c + P]
             words = (first, second)[h][:, e, a, c : c + P]
             return words.bitcast(FP8X4), plane
 
@@ -153,6 +156,16 @@ def tile_list_rgg_ownLP_kernel(
         def by_word(bank):
             return bank[:].rearrange("j (m t) -> j m t", t=PACK)
 
+        edge_weight = keep.tile([P, J // P], F32, name="edge_weight")
+        for h in range(2):
+            bank = psum.tile([P, 4, P], F32, name="turned")
+            for s in range(4):
+                b = 4 * h + s
+                nc.tensor.transpose(bank[:, s, :], weight[:, b * P : (b + 1) * P], ident[:])
+            nc.scalar.copy(edge_weight[:, 4 * h : 4 * h + 4], bank[:, :, 0])
+
+        residual = [keep.tile([P, J], F32, name="residual%d" % (t,)) for t in range(3)]
+        residual.append(residual[0])
         message = {}
         own = {}
 
@@ -168,82 +181,78 @@ def tile_list_rgg_ownLP_kernel(
 
             za = psum.tile([P, N], F32, name="za")
             group(za, [(e, a) + fp4(e, a) for a in range(PASSES) for e in range(2)])
-            ow = psum.tile([P, N], F32, name="ow", bufs=1)
+            ow = psum.tile([P, N], F32, name="ow")
             group(ow, [(0, a) + fp4(2, a) for a in range(PASSES)])
-            ms = psum.tile([P, N], F32, name="ms", bufs=3)
+            ms = psum.tile([P, N], F32, name="ms")
             group(ms, [(1, a, wc_codes[:, a, :].bitcast(FP8X4), wc_planes[:, a, :]) for a in range(PASSES)])
-            eta = keep.tile([P, PACK, P], F32, name="eta", bufs=4)
-            nc.scalar.activation(dealing(eta), by_word(za), SIGMOID)
+            if b % 4 == 3:
+                eta = residual[2][:, (b // 4) * HALF : (b // 4 + 1) * HALF]
+            else:
+                eta = keep.tile([P, N], F32, name="eta%d" % (b,))[:]
+            nc.scalar.activation(eta.rearrange("j (t m) -> j m t", t=PACK), by_word(za), SIGMOID)
             own[b] = keep.tile([P, PACK, P], F32, name="own%d" % (b,), tag="own%d" % (b,), align_bytes=64)
-            nc.scalar.copy(dealing(own[b]), by_word(ow))
+            nc.scalar.activation(dealing(own[b]), by_word(ow), COPY, scale=edge_weight[:, b : b + 1])
+            sent = keep.tile([P, N], F32, name="sent%d" % (b,))
+            nc.scalar.activation(sent[:], ms[:], COPY, scale=edge_weight[:, b : b + 1])
             message[b] = keep.tile([P, PACK, P], F32, name="message%d" % (b,))
-            nc.vector.tensor_tensor(message[b][:], ms[:].rearrange("j (t m) -> j t m", t=PACK), eta[:], MULT)
+            nc.vector.tensor_tensor(message[b][:].rearrange("j t m -> j (t m)"), sent[:], eta, MULT)
 
-        def turn(dst, parts):
-            bank = psum.tile([P, 4, P], F32, name="turned")
+        def turn(dst, parts, tag):
+            bank = psum.tile([P, 4, P], F32, name="turned", tag=tag)
             for s, (t, b) in enumerate(parts):
                 nc.tensor.matmul(bank[:, s, :], own[b][:, t, :], ident[:], start=True, stop=False, is_transpose=True)
                 nc.tensor.matmul(bank[:, s, :], message[b][:, t, :], ident[:], start=False, stop=True, is_transpose=True)
             nc.scalar.copy(dst, bank[:].rearrange("p s j -> p (s j)"))
 
-        def add_state(t, j0, j1, summed, name):
-            total = keep.tile([P, j1 - j0], F32, name=name)
-            nc.vector.tensor_tensor(total[:], state[t][:].indirect(offsets(dst_list, j0, j1)), summed, ADD)
-            return total
+        def gather_state(t, j0, j1):
+            nc.vector.tensor_tensor(residual[t][:, j0:j1], state[t][:].indirect(offsets(dst_list, j0, j1)), weight[:, j0:j1], MULT)
 
-        def scatter(t, j0, j1, total):
-            nc.vector.tensor_tensor(pages[t][:].indirect(offsets(dst_list, j0, j1)), total[:], weight[:, j0:j1], MULT)
+        summed = [keep.tile([P, J], F32, name="summed%d" % (t,)) for t in range(PACK)]
 
-        def early_pages(q):
-            summed = keep.tile([P, 2 * QUARTER], F32, name="summed", bufs=2)
-            turn(summed[:], [(t, b) for t in range(2) for b in (2 * q, 2 * q + 1)])
-            j0, j1 = q * QUARTER, (q + 1) * QUARTER
-            totals = [add_state(t, j0, j1, summed[:, t * QUARTER : (t + 1) * QUARTER], "total%d%d" % (t, q % 2,)) for t in range(2)]
-            for t in range(2):
-                scatter(t, j0, j1, totals[t])
+        def turn_half(t, h):
+            turn(summed[t][:, h * HALF : (h + 1) * HALF], [(t, b) for b in range(4 * h, 4 * h + 4)], "turned" if t == 0 else "ms")
 
-        products(0)
-        products(1)
-        products(2)
-        products(3)
-        early_pages(0)
-        products(4)
-        products(5)
-        early_pages(1)
-        products(6)
-        products(7)
-        early_pages(2)
-        early_pages(3)
-        for t in (2, 3):
-            summed = keep.tile([P, J], F32, name="summed_all%d" % (t,))
+        def scatter(t, j0, j1):
+            nc.vector.tensor_tensor(
+                pages[t % 2][:].indirect(offsets(dst_list, j0, j1)), residual[t][:, j0:j1], summed[t][:, j0:j1], ADD
+            )
+
+        gather_state(0, 0, J)
+        gather_state(1, 0, J)
+        for h in range(2):
+            j0, j1 = h * HALF, (h + 1) * HALF
+            for b in range(6 * h, 4 * h + 4):
+                products(b)
+            gather_state(2, j0, j1)
+            if h == 0:
+                products(4)
+                products(5)
+            turn_half(0, h)
+            scatter(0, j0, j1)
+            gather_state(3, j0, j1)
+        for t in range(1, PACK):
             for h in range(2):
-                turn(summed[:, h * HALF : (h + 1) * HALF], [(t, b) for b in range(4 * h, 4 * h + 4)])
-            scatter(t, 0, J, add_state(t, 0, J, summed[:], "total_all"))
+                turn_half(t, h)
 
         out_rows = out_0.rearrange("(p i) t -> p i t", i=PACK)
-        woven = keep.tile([P, T, PACK], BF16, name="woven", align_bytes=64)
-        for c in range(4):
-            cols = slice(c * CHUNK, (c + 1) * CHUNK)
-            pair = keep.tile([P, 2, CHUNK], F32, name="pair%d" % (c,))
-            for t in range(2):
-                nc.sync.dma_start(pair[:, t, :], pages[t][:, cols])
-            if c < 3:
-                nc.scalar.copy(woven[:, cols, 0:2], pair[:].rearrange("p t c -> p c t"))
-            else:
-                nc.scalar.copy(
-                    woven[:, cols, :].rearrange("p c (u t) -> p c u t", u=2),
-                    pair[:].rearrange("p t c -> p c t").unsqueeze(2).to_broadcast([P, CHUNK, 2, 2]),
-                )
-            nc.sync.dma_start(out_rows[:, 0:2, cols], pair[:])
-        for t in (2, 3):
-            nc.sync.dma_start(out_rows[:, t, :], pages[t][:])
-        nc.scalar.copy(woven[:, :, 2:4], pages[2][:].unsqueeze(2).to_broadcast([P, T, 2]))
+        woven = keep.tile([P, T, PACK], BF16, name="woven", tag="own7", align_bytes=64)
+        for t in range(PACK):
+            if t > 0:
+                scatter(t, 0, J)
+            nc.sync.dma_start(out_rows[:, t, :], pages[t % 2][:])
+            if t < 2:
+                nc.scalar.copy(woven[:, :, t], pages[t][:])
+            if t == 2:
+                seam = slice(CHUNK - EDGE, CHUNK + EDGE)
+                nc.scalar.copy(woven[:, : 2 * CHUNK, 2], pages[0][:, : 2 * CHUNK])
+                nc.scalar.copy(woven[:, seam, 2:4], pages[0][:, seam].unsqueeze(2).to_broadcast([P, 2 * EDGE, 2]))
+                nc.scalar.copy(woven[:, 2 * CHUNK :, 2], pages[0][:, 2 * CHUNK :])
         for c in range(4):
             cols = slice(c * CHUNK, (c + 1) * CHUNK)
             if c < 2:
-                nc.vector.tensor_copy(woven[:, cols, 3], pages[3][:, cols])
+                nc.vector.tensor_copy(woven[:, cols, 3], pages[1][:, cols])
             else:
-                nc.scalar.copy(woven[:, cols, 3], pages[3][:, cols])
+                nc.scalar.copy(woven[:, cols, 3], pages[1][:, cols])
         out_plane = keep.tile([P, T], U8, name="out_plane", align_bytes=64)
         out_words = out_1[0].rearrange("p t i -> p (t i)").bitcast(I32)
         for c in range(4):

@@ -46,7 +46,7 @@ def tile_list_rgg_ownLP_kernel(
             return lst[:, j0 // 16 : j1 // 16]
 
         tab_planes = keep.tile([P, T], U8, name="tab_planes", align_bytes=64)
-        nc.gpsimd.memset(tab_planes[:].bitcast(I32), 0)
+        nc.vector.memset(tab_planes[:].bitcast(I32), 0)
         w_planes = keep.tile([P, 3, PASSES, N], U8, name="w_planes", align_bytes=64)
         nc.vector.memset(w_planes[:].rearrange("p w a n -> p (w a n)").bitcast(I32), 0)
         moved = keep.tile([P, 2, 2, HALF], U8, name="moved", align_bytes=64)
@@ -125,15 +125,12 @@ def tile_list_rgg_ownLP_kernel(
         wc_codes = keep.tile([P, PASSES, N], U32, name="wc_codes", align_bytes=64)
         wc_planes = keep.tile([P, PASSES, N], U8, name="wc_planes", align_bytes=64)
         for a in range(PASSES):
-            grouped = keep.tile([P, PACK, P, PACK], BF16, name="grouped%d" % (a,), tag="hold_a%d" % (a,), align_bytes=64)
-            nc.scalar.copy(
-                grouped[:].rearrange("p t m i -> p m i t"),
-                wc_raw[a][:].rearrange("p i (m t) -> p m i t", t=PACK),
-            )
+            grouped = keep.tile([P, N, PACK], BF16, name="grouped%d" % (a,), tag="hold_a%d" % (a,), align_bytes=64)
+            nc.scalar.copy(grouped[:], wc_raw[a][:].rearrange("p i n -> p n i"))
             nc.vector.quantize_mx(
                 out=wc_codes[:, a, :].bitcast(FP8X4),
                 scales=wc_planes[:, a, :],
-                in_=grouped[:].rearrange("p t m i -> p (t m i)"),
+                in_=grouped[:].rearrange("p n i -> p (n i)"),
             )
             load_state(1 + a, "early%d" % (a,), 64)
 
@@ -192,10 +189,10 @@ def tile_list_rgg_ownLP_kernel(
             nc.scalar.activation(eta.rearrange("j (t m) -> j m t", t=PACK), by_word(za), SIGMOID)
             own[b] = keep.tile([P, PACK, P], F32, name="own%d" % (b,), tag="own%d" % (b,), align_bytes=64)
             nc.scalar.activation(dealing(own[b]), by_word(ow), COPY, scale=edge_weight[:, b : b + 1])
-            sent = keep.tile([P, N], F32, name="sent%d" % (b,))
-            nc.scalar.activation(sent[:], ms[:], COPY, scale=edge_weight[:, b : b + 1])
+            sent = keep.tile([P, PACK, P], F32, name="sent%d" % (b,))
+            nc.scalar.activation(dealing(sent), by_word(ms), COPY, scale=edge_weight[:, b : b + 1])
             message[b] = keep.tile([P, PACK, P], F32, name="message%d" % (b,))
-            nc.vector.tensor_tensor(message[b][:].rearrange("j t m -> j (t m)"), sent[:], eta, MULT)
+            nc.vector.tensor_tensor(message[b][:].rearrange("j t m -> j (t m)"), sent[:].rearrange("j t m -> j (t m)"), eta, MULT)
 
         def turn(dst, parts, tag):
             bank = psum.tile([P, 4, P], F32, name="turned", tag=tag)

@@ -49,8 +49,8 @@ def tile_list_rgg_ownLP_kernel(
         nc.vector.memset(tab_planes[:].bitcast(I32), 0)
         w_planes = keep.tile([P, 3, PASSES, N], U8, name="w_planes", align_bytes=64)
         nc.vector.memset(w_planes[:].rearrange("p w a n -> p (w a n)").bitcast(I32), 0)
-        moved = keep.tile([P, 2, 2, HALF], U8, name="moved", align_bytes=64)
-        nc.vector.memset(moved[:].rearrange("p h e j -> p (h e j)").bitcast(I32), 0)
+        moved = keep.tile([P, 2, J], U8, name="moved", align_bytes=64)
+        nc.vector.memset(moved[:].rearrange("p e j -> p (e j)").bitcast(I32), 0)
         pages = [keep.tile([P, T], F32, name="page%d" % (u,)) for u in range(2)]
         for u in range(2):
             nc.vector.memset(pages[u][:].bitcast(I32), 0)
@@ -68,12 +68,17 @@ def tile_list_rgg_ownLP_kernel(
             nc.sync.dma_start(wc_raw[a][:], wc[512 * a : 512 * (a + 1), :].rearrange("(p i) n -> p i n", i=PACK))
 
         nc.sync.dma_start(dst_list[:], offs2)
-        nc.sync.dma_start(src_list[:], offs)
         w_rows = keep.tile([16, 3, PASSES, N // 4], I32, name="w_rows", tag="w_rows", align_bytes=64)
-        for w, src in enumerate((wa_scales, wb_scales, wo_scales)):
+
+        def load_rows(w, src):
             nc.sync.dma_start(w_rows[:, w, :, :], src.rearrange("a q n -> q a n").bitcast(I32))
+
+        load_rows(0, wa_scales)
+        load_rows(1, wb_scales)
+        load_rows(2, wo_scales)
         for q in range(4):
             nc.sync.dma_start(tab_planes[32 * q : 32 * q + 8, :].bitcast(I32), tab_scales[:, 4 * q : 4 * q + 4, :].bitcast(I32))
+        nc.sync.dma_start(src_list[:], offs)
         load_table(0)
         for q in range(4):
             nc.sync.dma_start(
@@ -81,15 +86,15 @@ def tile_list_rgg_ownLP_kernel(
                 w_rows[4 * q : 4 * q + 4].rearrange("p w a n -> p (w a n)"),
             )
         load_wc(0)
-        load_wc(1)
         load_table(1)
+        load_wc(1)
+        weight = keep.tile([P, J], F32, name="weight", align_bytes=64)
+        nc.sync.dma_start(weight[:], wgo)
         w_words = []
         for w, src in enumerate((wa_words, wb_words, wo_words)):
             tile_w = keep.tile([P, PASSES, 2 * N], U8, name="w_words%d" % (w,), align_bytes=64)
             nc.sync.dma_start(tile_w[:].bitcast(I32), src.rearrange("a p b -> p a b").bitcast(I32))
             w_words.append(tile_w)
-        weight = keep.tile([P, J], F32, name="weight", align_bytes=64)
-        nc.sync.dma_start(weight[:], wgo)
         r_rows = rT.rearrange("(p i) t -> p i t", i=PACK)
         state = {}
 
@@ -99,24 +104,18 @@ def tile_list_rgg_ownLP_kernel(
 
         load_state(0, "w_rows", 64)
 
-        picked_planes = {}
-
-        def gather_planes(h):
-            g = keep.tile([P, 2, HALF], U8, name="picked_planes%d" % (h,), align_bytes=64)
-            for e in range(2):
-                nc.vector.tensor_copy(g[:, e, :], tab_planes[:].indirect(offsets(edge_lists[e], h * HALF, (h + 1) * HALF)))
-            nc.sync.dma_start(
-                moved[0:100, h].rearrange("p e j -> p (e j)").bitcast(I32),
-                g[4:104].rearrange("p e j -> p (e j)").bitcast(I32),
-            )
-            picked_planes[h] = g
+        picked_planes = keep.tile([P, 2, J], U8, name="picked_planes", align_bytes=64)
+        for e in range(2):
+            nc.vector.tensor_copy(picked_planes[:, e, :], tab_planes[:].indirect(edge_lists[e][:]))
+        nc.sync.dma_start(
+            moved[0:100].rearrange("p e j -> p (e j)").bitcast(I32),
+            picked_planes[4:104].rearrange("p e j -> p (e j)").bitcast(I32),
+        )
 
         def gather_words(dst, e, a, j0, j1):
             nc.vector.tensor_copy(dst, table[a][:].bitcast(U32).indirect(offsets(edge_lists[e], j0, j1)))
 
         first = keep.tile([P, 2, PASSES, HALF], U32, name="first", align_bytes=64)
-        gather_planes(0)
-        gather_planes(1)
         gather_words(first[:, 0, 0, :], 0, 0, 0, HALF)
         gather_words(first[:, 1, 0, :], 1, 0, 0, HALF)
         gather_words(first[:, 0, 1, :], 0, 1, 0, HALF)
@@ -134,17 +133,18 @@ def tile_list_rgg_ownLP_kernel(
             )
             load_state(1 + a, "early%d" % (a,), 64)
 
-        second = keep.tile([P, 2, PASSES, HALF], U32, name="second", tag="hold_a1", align_bytes=64)
+        second = []
         for a in range(PASSES):
+            second.append(keep.tile([P, 2, HALF], U32, name="second%d" % (a,), tag="hold_a%d" % (a,), align_bytes=64))
             for e in range(2):
-                gather_words(second[:, e, a, :], e, a, HALF, J)
+                gather_words(second[a][:, e, :], e, a, HALF, J)
         load_state(3, "late1", 64)
 
 
         def picked(b, e, a):
             h, c = divmod(b * P, HALF)
-            plane = picked_planes[h][:, e, c : c + P] if a == 0 else moved[:, h, e, c : c + P]
-            words = (first, second)[h][:, e, a, c : c + P]
+            plane = (picked_planes, moved)[a][:, e, b * P : (b + 1) * P]
+            words = first[:, e, a, c : c + P] if h == 0 else second[a][:, e, c : c + P]
             return words.bitcast(FP8X4), plane
 
         def dealing(tile):
@@ -162,7 +162,7 @@ def tile_list_rgg_ownLP_kernel(
             nc.scalar.copy(edge_weight[:, 4 * h : 4 * h + 4], bank[:, :, 0])
 
         residual = [keep.tile([P, J], F32, name="residual%d" % (t,)) for t in range(3)]
-        residual.append(residual[0])
+        residual.append(residual[1])
         message = {}
         own = {}
 
@@ -207,7 +207,7 @@ def tile_list_rgg_ownLP_kernel(
         summed = [keep.tile([P, J], F32, name="summed%d" % (t,)) for t in range(PACK)]
 
         def turn_half(t, h):
-            turn(summed[t][:, h * HALF : (h + 1) * HALF], [(t, b) for b in range(4 * h, 4 * h + 4)], "turned" if t == 0 else "ms")
+            turn(summed[t][:, h * HALF : (h + 1) * HALF], [(t, b) for b in range(4 * h, 4 * h + 4)], "turned" if t < 2 else "ms")
 
         def scatter(t, j0, j1):
             nc.vector.tensor_tensor(
@@ -218,32 +218,36 @@ def tile_list_rgg_ownLP_kernel(
         gather_state(1, 0, J)
         for h in range(2):
             j0, j1 = h * HALF, (h + 1) * HALF
-            for b in range(6 * h, 4 * h + 4):
+            for b in range(5 * h, 4 * h + 4):
                 products(b)
             gather_state(2, j0, j1)
             if h == 0:
                 products(4)
-                products(5)
-            turn_half(0, h)
-            scatter(0, j0, j1)
-            gather_state(3, j0, j1)
-        for t in range(1, PACK):
+            for t in range(2):
+                turn_half(t, h)
+                scatter(t, j0, j1)
+        gather_state(3, 0, J)
+        for t in range(2, PACK):
             for h in range(2):
                 turn_half(t, h)
 
         out_rows = out_0.rearrange("(p i) t -> p i t", i=PACK)
-        woven = keep.tile([P, T, PACK], BF16, name="woven", tag="own7", align_bytes=64)
+        woven = keep.tile([P, T, PACK], BF16, name="woven", tag="late0", align_bytes=64)
+        rounded = keep.tile([P, 2, T], BF16, name="rounded", tag="own7", align_bytes=64)
         for t in range(PACK):
-            if t > 0:
+            if t > 1:
                 scatter(t, 0, J)
             nc.sync.dma_start(out_rows[:, t, :], pages[t % 2][:])
             if t < 2:
-                nc.scalar.copy(woven[:, :, t], pages[t][:])
+                nc.scalar.copy(rounded[:, t, :], pages[t][:])
+            if t == 1:
+                nc.scalar.copy(woven[:, : T - EDGE, 0:2], rounded[:, :, : T - EDGE].rearrange("p t c -> p c t"))
+                nc.scalar.copy(
+                    woven[:, T - EDGE :, :].rearrange("p c (u t) -> p c u t", u=2),
+                    rounded[:, :, T - EDGE :].rearrange("p t c -> p c t").unsqueeze(2).to_broadcast([P, EDGE, 2, 2]),
+                )
             if t == 2:
-                seam = slice(CHUNK - EDGE, CHUNK + EDGE)
-                nc.scalar.copy(woven[:, : 2 * CHUNK, 2], pages[0][:, : 2 * CHUNK])
-                nc.scalar.copy(woven[:, seam, 2:4], pages[0][:, seam].unsqueeze(2).to_broadcast([P, 2 * EDGE, 2]))
-                nc.scalar.copy(woven[:, 2 * CHUNK :, 2], pages[0][:, 2 * CHUNK :])
+                nc.scalar.copy(woven[:, :, 2:4], pages[0][:].unsqueeze(2).to_broadcast([P, T, 2]))
         for c in range(4):
             cols = slice(c * CHUNK, (c + 1) * CHUNK)
             if c < 2:

@@ -26,6 +26,7 @@ HALF = J // 2
 QUARTER = J // 4
 CHUNK = 512
 EDGE = 8
+SPLIT = 1152
 
 
 def tile_list_rgg_ownLP_kernel(
@@ -76,8 +77,11 @@ def tile_list_rgg_ownLP_kernel(
         load_rows(0, wa_scales)
         load_rows(1, wb_scales)
         load_rows(2, wo_scales)
-        for q in range(4):
-            nc.sync.dma_start(tab_planes[32 * q : 32 * q + 8, :].bitcast(I32), tab_scales[:, 4 * q : 4 * q + 4, :].bitcast(I32))
+        for r in range(4):
+            nc.sync.dma_start(
+                tab_planes[r:P:16, :].bitcast(I32),
+                tab_scales.rearrange("a (q r) t -> r q a t", r=4)[r].bitcast(I32),
+            )
         nc.sync.dma_start(src_list[:], offs)
         load_table(0)
         for q in range(4):
@@ -109,7 +113,7 @@ def tile_list_rgg_ownLP_kernel(
             nc.vector.tensor_copy(picked_planes[:, e, :], tab_planes[:].indirect(edge_lists[e][:]))
         nc.sync.dma_start(
             moved[0:100].rearrange("p e j -> p (e j)").bitcast(I32),
-            picked_planes[4:104].rearrange("p e j -> p (e j)").bitcast(I32),
+            picked_planes[16:116].rearrange("p e j -> p (e j)").bitcast(I32),
         )
 
         def gather_words(dst, e, a, j0, j1):
@@ -131,11 +135,11 @@ def tile_list_rgg_ownLP_kernel(
                 scales=wc_planes[:, a, :],
                 in_=grouped[:].rearrange("p n i -> p (n i)"),
             )
-            load_state(1 + a, "early%d" % (a,), 64)
+            load_state(1 + a, "state%d" % (1 + a,), 64)
 
         second = []
         for a in range(PASSES):
-            second.append(keep.tile([P, 2, HALF], U32, name="second%d" % (a,), tag="hold_a%d" % (a,), align_bytes=64))
+            second.append(keep.tile([P, 2, HALF], U32, name="second%d" % (a,), tag="early%d" % (a,), align_bytes=64))
             for e in range(2):
                 gather_words(second[a][:, e, :], e, a, HALF, J)
         load_state(3, "late1", 64)
@@ -162,7 +166,7 @@ def tile_list_rgg_ownLP_kernel(
             nc.scalar.copy(edge_weight[:, 4 * h : 4 * h + 4], bank[:, :, 0])
 
         residual = [keep.tile([P, J], F32, name="residual%d" % (t,)) for t in range(3)]
-        residual.append(residual[1])
+        residual.append(residual[0])
         message = {}
         own = {}
 
@@ -241,19 +245,20 @@ def tile_list_rgg_ownLP_kernel(
             if t < 2:
                 nc.scalar.copy(rounded[:, t, :], pages[t][:])
             if t == 1:
-                nc.scalar.copy(woven[:, : T - EDGE, 0:2], rounded[:, :, : T - EDGE].rearrange("p t c -> p c t"))
+                border = slice(SPLIT - EDGE, SPLIT + EDGE)
+                for cols in (slice(0, border.start), slice(border.stop, T)):
+                    nc.scalar.copy(woven[:, cols, 0:2], rounded[:, :, cols].rearrange("p t c -> p c t"))
                 nc.scalar.copy(
-                    woven[:, T - EDGE :, :].rearrange("p c (u t) -> p c u t", u=2),
-                    rounded[:, :, T - EDGE :].rearrange("p t c -> p c t").unsqueeze(2).to_broadcast([P, EDGE, 2, 2]),
+                    woven[:, border, :].rearrange("p c (u t) -> p c u t", u=2),
+                    rounded[:, :, border].rearrange("p t c -> p c t").unsqueeze(2).to_broadcast([P, 2 * EDGE, 2, 2]),
                 )
             if t == 2:
-                nc.scalar.copy(woven[:, :, 2:4], pages[0][:].unsqueeze(2).to_broadcast([P, T, 2]))
-        for c in range(4):
-            cols = slice(c * CHUNK, (c + 1) * CHUNK)
-            if c < 2:
-                nc.vector.tensor_copy(woven[:, cols, 3], pages[1][:, cols])
-            else:
-                nc.scalar.copy(woven[:, cols, 3], pages[1][:, cols])
+                for c0, c1 in ((0, SPLIT), (SPLIT, T)):
+                    nc.scalar.copy(woven[:, c0:c1, 2:4], pages[0][:, c0:c1].unsqueeze(2).to_broadcast([P, c1 - c0, 2]))
+        for c0, c1 in ((0, CHUNK), (CHUNK, SPLIT)):
+            nc.vector.tensor_copy(woven[:, c0:c1, 3], pages[1][:, c0:c1])
+        for c0, c1 in ((SPLIT, T - CHUNK), (T - CHUNK, T)):
+            nc.scalar.copy(woven[:, c0:c1, 3], pages[1][:, c0:c1])
         out_plane = keep.tile([P, T], U8, name="out_plane", align_bytes=64)
         out_words = out_1[0].rearrange("p t i -> p (t i)").bitcast(I32)
         for c in range(4):

@@ -37,6 +37,7 @@ def tile_list_rgg_ownLP_kernel(
     with ExitStack() as ctx:
         lists = ctx.enter_context(tc.tile_pool(name="lists", bufs=1))
         keep = ctx.enter_context(tc.tile_pool(name="keep", bufs=1))
+        placed = ctx.enter_context(tc.tile_pool(name="placed", bufs=1))
         psum = ctx.enter_context(tc.psum_pool(name="psum", bufs=2))
 
         src_list = lists.tile([P, J // 16], U16, name="src_list")
@@ -46,7 +47,7 @@ def tile_list_rgg_ownLP_kernel(
         def offsets(lst, j0, j1):
             return lst[:, j0 // 16 : j1 // 16]
 
-        tab_planes = keep.tile([P, T], U8, name="tab_planes", align_bytes=64)
+        tab_planes = placed.tile([P, T], U8, name="tab_planes", align_bytes=64, offset=5632)
         nc.vector.memset(tab_planes[:].bitcast(I32), 0)
         w_planes = keep.tile([P, 3, PASSES, N], U8, name="w_planes", align_bytes=64)
         nc.vector.memset(w_planes[:].rearrange("p w a n -> p (w a n)").bitcast(I32), 0)
@@ -55,6 +56,8 @@ def tile_list_rgg_ownLP_kernel(
         pages = [keep.tile([P, T], F32, name="page%d" % (u,)) for u in range(2)]
         for u in range(2):
             nc.vector.memset(pages[u][:].bitcast(I32), 0)
+        weight_rows = keep.tile([P, P], F32, name="weight_rows")
+        nc.vector.memset(weight_rows[:], 0.0)
         ident = keep.tile([P, P], F32, name="ident")
         make_identity(nc, ident[:])
 
@@ -63,9 +66,10 @@ def tile_list_rgg_ownLP_kernel(
         def load_table(a):
             nc.sync.dma_start(table[a][:], tab_words[a].rearrange("p t i -> p (t i)").bitcast(I32))
 
-        wc_raw = [keep.tile([P, PACK, N], F32, name="wc_raw%d" % (a,), tag="early%d" % (a,), align_bytes=64) for a in range(PASSES)]
+        wc_raw = {}
 
-        def load_wc(a):
+        def load_wc(a, tile):
+            wc_raw[a] = tile
             nc.sync.dma_start(wc_raw[a][:], wc[512 * a : 512 * (a + 1), :].rearrange("(p i) n -> p i n", i=PACK))
 
         nc.sync.dma_start(dst_list[:], offs2)
@@ -83,22 +87,16 @@ def tile_list_rgg_ownLP_kernel(
                 tab_scales.rearrange("a (q r) t -> r q a t", r=4)[r].bitcast(I32),
             )
         nc.sync.dma_start(src_list[:], offs)
+        nc.sync.dma_start(weight_rows[0 : J // P, :], wgo[0].rearrange("(b j) -> b j", j=P))
         load_table(0)
         for q in range(4):
             nc.sync.dma_start(
                 w_planes[32 * q : 32 * q + 4].rearrange("p w a n -> p (w a n)").bitcast(I32),
                 w_rows[4 * q : 4 * q + 4].rearrange("p w a n -> p (w a n)"),
             )
-        load_wc(0)
+        load_wc(0, keep.tile([P, PACK, N], F32, name="wc_raw0", tag="early0", align_bytes=64))
         load_table(1)
-        load_wc(1)
-        weight = keep.tile([P, J], F32, name="weight", align_bytes=64)
-        nc.sync.dma_start(weight[:], wgo)
-        w_words = []
-        for w, src in enumerate((wa_words, wb_words, wo_words)):
-            tile_w = keep.tile([P, PASSES, 2 * N], U8, name="w_words%d" % (w,), align_bytes=64)
-            nc.sync.dma_start(tile_w[:].bitcast(I32), src.rearrange("a p b -> p a b").bitcast(I32))
-            w_words.append(tile_w)
+        load_wc(1, keep.tile([P, PACK, N], F32, name="wc_raw1", tag="early1", align_bytes=64))
         r_rows = rT.rearrange("(p i) t -> p i t", i=PACK)
         state = {}
 
@@ -106,7 +104,6 @@ def tile_list_rgg_ownLP_kernel(
             state[t] = keep.tile([P, T], F32, name="state%d" % (t,), tag=tag, align_bytes=align)
             nc.sync.dma_start(state[t][:], r_rows[:, t, :])
 
-        load_state(0, "w_rows", 64)
 
         picked_planes = keep.tile([P, 2, J], U8, name="picked_planes", align_bytes=64)
         for e in range(2):
@@ -115,6 +112,12 @@ def tile_list_rgg_ownLP_kernel(
             moved[0:100].rearrange("p e j -> p (e j)").bitcast(I32),
             picked_planes[16:116].rearrange("p e j -> p (e j)").bitcast(I32),
         )
+
+        w_words = placed.tile([P, 3, PASSES, 2 * N], U8, name="w_words", align_bytes=64, offset=0)
+        for w, src in enumerate((wa_words, wb_words, wo_words)):
+            nc.sync.dma_start(w_words[:, w].bitcast(I32), src.rearrange("a p b -> p a b").bitcast(I32))
+        state[0] = placed.tile([P, T], F32, name="state0", align_bytes=64, offset=7168)
+        nc.sync.dma_start(state[0][:], r_rows[:, 0, :])
 
         def gather_words(dst, e, a, j0, j1):
             nc.vector.tensor_copy(dst, table[a][:].bitcast(U32).indirect(offsets(edge_lists[e], j0, j1)))
@@ -135,8 +138,9 @@ def tile_list_rgg_ownLP_kernel(
                 scales=wc_planes[:, a, :],
                 in_=grouped[:].rearrange("p n i -> p (n i)"),
             )
-            load_state(1 + a, "state%d" % (1 + a,), 64)
 
+        load_state(1, "hold_a0", 64)
+        load_state(2, "hold_a1", 64)
         second = []
         for a in range(PASSES):
             second.append(keep.tile([P, 2, HALF], U32, name="second%d" % (a,), tag="early%d" % (a,), align_bytes=64))
@@ -158,45 +162,57 @@ def tile_list_rgg_ownLP_kernel(
             return bank[:].rearrange("j (m t) -> j m t", t=PACK)
 
         edge_weight = keep.tile([P, J // P], F32, name="edge_weight")
+        bank = psum.tile([P, P], F32, name="turned")
+        nc.tensor.transpose(bank[:], weight_rows[:], ident[:])
+        nc.scalar.copy(edge_weight[:], bank[:, 0 : J // P])
+        weight = keep.tile([P, J], F32, name="weight", align_bytes=64)
         for h in range(2):
             bank = psum.tile([P, 4, P], F32, name="turned")
             for s in range(4):
                 b = 4 * h + s
-                nc.tensor.transpose(bank[:, s, :], weight[:, b * P : (b + 1) * P], ident[:])
-            nc.scalar.copy(edge_weight[:, 4 * h : 4 * h + 4], bank[:, :, 0])
+                nc.tensor.transpose(bank[:, s, :], edge_weight[:, b : b + 1].to_broadcast([P, P]), ident[:])
+            nc.scalar.copy(weight[:, h * HALF : (h + 1) * HALF], bank[:].rearrange("p s j -> p (s j)"))
 
         residual = [keep.tile([P, J], F32, name="residual%d" % (t,)) for t in range(3)]
         residual.append(residual[0])
         message = {}
         own = {}
 
-        def products(b):
-            def group(bank, terms):
-                for i, (e, a, rhs, rhs_plane) in enumerate(terms):
-                    words, plane = picked(b, e, a)
-                    nc.tensor.matmul_mx(out=bank[:], lhsT=words, lhsT_scale=plane, rhs=rhs, rhs_scale=rhs_plane,
-                                        start=(i == 0), stop=(i == len(terms) - 1))
+        gate = {}
 
-            def fp4(w, a):
-                return w_words[w][:, a, :].bitcast(FP4X4), w_planes[:, w, a, :]
+        def group(b, bank, terms):
+            for i, (e, a, rhs, rhs_plane) in enumerate(terms):
+                words, plane = picked(b, e, a)
+                nc.tensor.matmul_mx(out=bank[:], lhsT=words, lhsT_scale=plane, rhs=rhs, rhs_scale=rhs_plane,
+                                    start=(i == 0), stop=(i == len(terms) - 1))
 
+        def fp4(w, a):
+            return w_words[:, w, a, :].bitcast(FP4X4), w_planes[:, w, a, :]
+
+        def packed_products(b):
             za = psum.tile([P, N], F32, name="za")
-            group(za, [(e, a) + fp4(e, a) for a in range(PASSES) for e in range(2)])
+            group(b, za, [(e, a) + fp4(e, a) for a in range(PASSES) for e in range(2)])
             ow = psum.tile([P, N], F32, name="ow")
-            group(ow, [(0, a) + fp4(2, a) for a in range(PASSES)])
-            ms = psum.tile([P, N], F32, name="ms")
-            group(ms, [(1, a, wc_codes[:, a, :].bitcast(FP8X4), wc_planes[:, a, :]) for a in range(PASSES)])
+            group(b, ow, [(0, a) + fp4(2, a) for a in range(PASSES)])
             if b % 4 == 3:
-                eta = residual[2][:, (b // 4) * HALF : (b // 4 + 1) * HALF]
+                gate[b] = residual[2][:, (b // 4) * HALF : (b // 4 + 1) * HALF]
             else:
-                eta = keep.tile([P, N], F32, name="eta%d" % (b,))[:]
-            nc.scalar.activation(eta.rearrange("j (t m) -> j m t", t=PACK), by_word(za), SIGMOID)
+                gate[b] = keep.tile([P, N], F32, name="eta%d" % (b,))[:]
+            nc.scalar.activation(gate[b].rearrange("j (t m) -> j m t", t=PACK), by_word(za), SIGMOID)
             own[b] = keep.tile([P, PACK, P], F32, name="own%d" % (b,), tag="own%d" % (b,), align_bytes=64)
             nc.scalar.activation(dealing(own[b]), by_word(ow), COPY, scale=edge_weight[:, b : b + 1])
+
+        def gated_message(b):
+            ms = psum.tile([P, N], F32, name="ms")
+            group(b, ms, [(1, a, wc_codes[:, a, :].bitcast(FP8X4), wc_planes[:, a, :]) for a in range(PASSES)])
             sent = keep.tile([P, PACK, P], F32, name="sent%d" % (b,))
             nc.scalar.activation(dealing(sent), by_word(ms), COPY, scale=edge_weight[:, b : b + 1])
             message[b] = keep.tile([P, PACK, P], F32, name="message%d" % (b,))
-            nc.vector.tensor_tensor(message[b][:].rearrange("j t m -> j (t m)"), sent[:].rearrange("j t m -> j (t m)"), eta, MULT)
+            nc.vector.tensor_tensor(message[b][:].rearrange("j t m -> j (t m)"), sent[:].rearrange("j t m -> j (t m)"), gate[b], MULT)
+
+        def products(b):
+            packed_products(b)
+            gated_message(b)
 
         def turn(dst, parts, tag):
             bank = psum.tile([P, 4, P], F32, name="turned", tag=tag)

@@ -25,8 +25,9 @@ PASSES = 2
 HALF = J // 2
 QUARTER = J // 4
 CHUNK = 512
-EDGE = 8
+ORDER = (0, 2, 1, 3)
 SPLIT = 1152
+LEAD = 256
 
 
 def tile_list_rgg_ownLP_kernel(
@@ -102,7 +103,7 @@ def tile_list_rgg_ownLP_kernel(
 
         def load_state(t, tag, align):
             state[t] = keep.tile([P, T], F32, name="state%d" % (t,), tag=tag, align_bytes=align)
-            nc.sync.dma_start(state[t][:], r_rows[:, t, :])
+            nc.sync.dma_start(state[t][:], r_rows[:, ORDER[t], :])
 
 
         picked_planes = keep.tile([P, 2, J], U8, name="picked_planes", align_bytes=64)
@@ -174,7 +175,6 @@ def tile_list_rgg_ownLP_kernel(
             nc.scalar.copy(weight[:, h * HALF : (h + 1) * HALF], bank[:].rearrange("p s j -> p (s j)"))
 
         residual = [keep.tile([P, J], F32, name="residual%d" % (t,)) for t in range(3)]
-        residual.append(residual[0])
         message = {}
         own = {}
 
@@ -199,7 +199,10 @@ def tile_list_rgg_ownLP_kernel(
             else:
                 gate[b] = keep.tile([P, N], F32, name="eta%d" % (b,))[:]
             nc.scalar.activation(gate[b].rearrange("j (t m) -> j m t", t=PACK), by_word(za), SIGMOID)
-            own[b] = keep.tile([P, PACK, P], F32, name="own%d" % (b,), tag="own%d" % (b,), align_bytes=64)
+            if b == 7:
+                own[b] = placed.tile([P, PACK, P], F32, name="own7", align_bytes=64, offset=18944)
+            else:
+                own[b] = keep.tile([P, PACK, P], F32, name="own%d" % (b,), tag="own%d" % (b,), align_bytes=64)
             nc.scalar.activation(dealing(own[b]), by_word(ow), COPY, scale=edge_weight[:, b : b + 1])
 
         def gated_message(b):
@@ -217,22 +220,22 @@ def tile_list_rgg_ownLP_kernel(
         def turn(dst, parts, tag):
             bank = psum.tile([P, 4, P], F32, name="turned", tag=tag)
             for s, (t, b) in enumerate(parts):
-                nc.tensor.matmul(bank[:, s, :], own[b][:, t, :], ident[:], start=True, stop=False, is_transpose=True)
-                nc.tensor.matmul(bank[:, s, :], message[b][:, t, :], ident[:], start=False, stop=True, is_transpose=True)
+                nc.tensor.matmul(bank[:, s, :], own[b][:, ORDER[t], :], ident[:], start=True, stop=False, is_transpose=True)
+                nc.tensor.matmul(bank[:, s, :], message[b][:, ORDER[t], :], ident[:], start=False, stop=True, is_transpose=True)
             nc.scalar.copy(dst, bank[:].rearrange("p s j -> p (s j)"))
 
-        def gather_state(t, j0, j1):
-            nc.vector.tensor_tensor(residual[t][:, j0:j1], state[t][:].indirect(offsets(dst_list, j0, j1)), weight[:, j0:j1], MULT)
+        def gather_state(t, j0, j1, out=None):
+            out = residual[t][:, j0:j1] if out is None else out
+            nc.vector.tensor_tensor(out, state[t][:].indirect(offsets(dst_list, j0, j1)), weight[:, j0:j1], MULT)
 
         summed = [keep.tile([P, J], F32, name="summed%d" % (t,)) for t in range(PACK)]
 
         def turn_half(t, h):
             turn(summed[t][:, h * HALF : (h + 1) * HALF], [(t, b) for b in range(4 * h, 4 * h + 4)], "turned" if t < 2 else "ms")
 
-        def scatter(t, j0, j1):
-            nc.vector.tensor_tensor(
-                pages[t % 2][:].indirect(offsets(dst_list, j0, j1)), residual[t][:, j0:j1], summed[t][:, j0:j1], ADD
-            )
+        def scatter(t, j0, j1, part=None):
+            part = residual[t][:, j0:j1] if part is None else part
+            nc.vector.tensor_tensor(pages[t % 2][:].indirect(offsets(dst_list, j0, j1)), part, summed[t][:, j0:j1], ADD)
 
         gather_state(0, 0, J)
         gather_state(1, 0, J)
@@ -246,31 +249,36 @@ def tile_list_rgg_ownLP_kernel(
             for t in range(2):
                 turn_half(t, h)
                 scatter(t, j0, j1)
-        gather_state(3, 0, J)
+        gather_state(3, 0, HALF, residual[0][:, HALF:J])
         for t in range(2, PACK):
             for h in range(2):
                 turn_half(t, h)
 
         out_rows = out_0.rearrange("(p i) t -> p i t", i=PACK)
         woven = keep.tile([P, T, PACK], BF16, name="woven", tag="late0", align_bytes=64)
-        rounded = keep.tile([P, 2, T], BF16, name="rounded", tag="own7", align_bytes=64)
-        for t in range(PACK):
-            if t > 1:
-                scatter(t, 0, J)
-            nc.sync.dma_start(out_rows[:, t, :], pages[t % 2][:])
-            if t < 2:
-                nc.scalar.copy(rounded[:, t, :], pages[t][:])
-            if t == 1:
-                border = slice(SPLIT - EDGE, SPLIT + EDGE)
-                for cols in (slice(0, border.start), slice(border.stop, T)):
-                    nc.scalar.copy(woven[:, cols, 0:2], rounded[:, :, cols].rearrange("p t c -> p c t"))
-                nc.scalar.copy(
-                    woven[:, border, :].rearrange("p c (u t) -> p c u t", u=2),
-                    rounded[:, :, border].rearrange("p t c -> p c t").unsqueeze(2).to_broadcast([P, 2 * EDGE, 2, 2]),
-                )
-            if t == 2:
-                for c0, c1 in ((0, SPLIT), (SPLIT, T)):
-                    nc.scalar.copy(woven[:, c0:c1, 2:4], pages[0][:, c0:c1].unsqueeze(2).to_broadcast([P, c1 - c0, 2]))
+        parts = ((0, LEAD), (LEAD, SPLIT), (SPLIT, T))
+        rounded = [
+            placed.tile([P, 2, c1 - c0], BF16, name="rounded%d" % (k,), align_bytes=64, offset=(19456, 20480, 15872)[k])
+            for k, (c0, c1) in enumerate(parts)
+        ]
+        for t in range(2):
+            nc.sync.dma_start(out_rows[:, ORDER[t], :], pages[t][:])
+            for k, (c0, c1) in enumerate(parts):
+                if (t, k) != (1, 0):
+                    nc.scalar.copy(rounded[k][:, t, :], pages[t][:, c0:c1])
+                else:
+                    nc.vector.tensor_copy(rounded[k][:, t, :], pages[t][:, c0:c1])
+        for k, (c0, c1) in enumerate(parts):
+            nc.scalar.copy(woven[:, c0:c1, 0:PACK:2], rounded[k][:].rearrange("p t c -> p c t"))
+        scatter(2, 0, J)
+        nc.sync.dma_start(out_rows[:, ORDER[2], :], pages[0][:])
+        for c0, c1 in ((0, SPLIT), (SPLIT, T)):
+            nc.scalar.copy(woven[:, c0:c1, 1], pages[0][:, c0:c1])
+        last = placed.tile([P, HALF], F32, name="residual3", align_bytes=64, offset=19456)
+        gather_state(3, HALF, J, last[:])
+        scatter(3, 0, HALF, residual[0][:, HALF:J])
+        scatter(3, HALF, J, last[:])
+        nc.sync.dma_start(out_rows[:, ORDER[3], :], pages[1][:])
         for c0, c1 in ((0, CHUNK), (CHUNK, SPLIT)):
             nc.vector.tensor_copy(woven[:, c0:c1, 3], pages[1][:, c0:c1])
         for c0, c1 in ((SPLIT, T - CHUNK), (T - CHUNK, T)):

from contextlib import ExitStack

import concourse.mybir as mybir
from concourse.masks import make_identity

K, N, T, J = 1024, 512, 2048, 1024
FLOPS = 4 * 2 * K * N * J

F32 = mybir.dt.float32
BF16 = mybir.dt.bfloat16
I32 = mybir.dt.int32
U32 = mybir.dt.uint32
U16 = mybir.dt.uint16
U8 = mybir.dt.uint8
FP8X4 = mybir.dt.float8_e4m3fn_x4
FP4X4 = mybir.dt.float4_e2m1fn_x4
MULT = mybir.AluOpType.mult
ADD = mybir.AluOpType.add
SIGMOID = mybir.ActivationFunctionType.Sigmoid
COPY = mybir.ActivationFunctionType.Copy

P = 128
PACK = 4
PASSES = 2
HALF = J // 2
QUARTER = J // 4
CHUNK = 512
ORDER = (0, 2, 1, 3)
SPLIT = 1152
LEAD = 256


def tile_list_rgg_ownLP_kernel(
    tc, tab_words, tab_scales, wa_words, wa_scales, wb_words, wb_scales, wc, wo_words, wo_scales,
    rT, wgo, offs, offs2, out_0, out_1, out_2,
):
    nc = tc.nc
    with ExitStack() as ctx:
        lists = ctx.enter_context(tc.tile_pool(name="lists", bufs=1))
        keep = ctx.enter_context(tc.tile_pool(name="keep", bufs=1))
        placed = ctx.enter_context(tc.tile_pool(name="placed", bufs=1))
        psum = ctx.enter_context(tc.psum_pool(name="psum", bufs=2))

        src_list = lists.tile([P, J // 16], U16, name="src_list")
        dst_list = lists.tile([P, J // 16], U16, name="dst_list")
        edge_lists = (dst_list, src_list)

        def offsets(lst, j0, j1):
            return lst[:, j0 // 16 : j1 // 16]

        tab_planes = placed.tile([P, T], U8, name="tab_planes", align_bytes=64, offset=5632)
        nc.vector.memset(tab_planes[:].bitcast(I32), 0)
        w_planes = keep.tile([P, 3, PASSES, N], U8, name="w_planes", align_bytes=64)
        nc.vector.memset(w_planes[:].rearrange("p w a n -> p (w a n)").bitcast(I32), 0)
        moved = keep.tile([P, 2, J], U8, name="moved", align_bytes=64)
        nc.vector.memset(moved[:].rearrange("p e j -> p (e j)").bitcast(I32), 0)
        pages = [keep.tile([P, T], F32, name="page%d" % (u,)) for u in range(2)]
        for u in range(2):
            nc.vector.memset(pages[u][:].bitcast(I32), 0)
        weight_rows = keep.tile([P, P], F32, name="weight_rows")
        nc.vector.memset(weight_rows[:], 0.0)
        ident = keep.tile([P, P], F32, name="ident")
        make_identity(nc, ident[:])

        table = [keep.tile([P, T], I32, name="table%d" % (a,), tag="late%d" % (a,), align_bytes=64) for a in range(PASSES)]

        def load_table(a):
            nc.sync.dma_start(table[a][:], tab_words[a].rearrange("p t i -> p (t i)").bitcast(I32))

        wc_raw = {}

        def load_wc(a, tile):
            wc_raw[a] = tile
            nc.sync.dma_start(wc_raw[a][:], wc[512 * a : 512 * (a + 1), :].rearrange("(p i) n -> p i n", i=PACK))

        nc.sync.dma_start(dst_list[:], offs2)
        w_rows = keep.tile([16, 3, PASSES, N // 4], I32, name="w_rows", tag="w_rows", align_bytes=64)

        def load_rows(w, src):
            nc.sync.dma_start(w_rows[:, w, :, :], src.rearrange("a q n -> q a n").bitcast(I32))

        load_rows(0, wa_scales)
        load_rows(1, wb_scales)
        load_rows(2, wo_scales)
        for r in range(4):
            nc.sync.dma_start(
                tab_planes[r:P:16, :].bitcast(I32),
                tab_scales.rearrange("a (q r) t -> r q a t", r=4)[r].bitcast(I32),
            )
        nc.sync.dma_start(src_list[:], offs)
        nc.sync.dma_start(weight_rows[0 : J // P, :], wgo[0].rearrange("(b j) -> b j", j=P))
        load_table(0)
        for q in range(4):
            nc.sync.dma_start(
                w_planes[32 * q : 32 * q + 4].rearrange("p w a n -> p (w a n)").bitcast(I32),
                w_rows[4 * q : 4 * q + 4].rearrange("p w a n -> p (w a n)"),
            )
        load_wc(0, keep.tile([P, PACK, N], F32, name="wc_raw0", tag="early0", align_bytes=64))
        load_table(1)
        load_wc(1, keep.tile([P, PACK, N], F32, name="wc_raw1", tag="early1", align_bytes=64))
        r_rows = rT.rearrange("(p i) t -> p i t", i=PACK)
        state = {}

        def load_state(t, tag, align):
            state[t] = keep.tile([P, T], F32, name="state%d" % (t,), tag=tag, align_bytes=align)
            nc.sync.dma_start(state[t][:], r_rows[:, ORDER[t], :])


        picked_planes = keep.tile([P, 2, J], U8, name="picked_planes", align_bytes=64)
        for e in range(2):
            nc.vector.tensor_copy(picked_planes[:, e, :], tab_planes[:].indirect(edge_lists[e][:]))
        nc.sync.dma_start(
            moved[0:100].rearrange("p e j -> p (e j)").bitcast(I32),
            picked_planes[16:116].rearrange("p e j -> p (e j)").bitcast(I32),
        )

        w_words = placed.tile([P, 3, PASSES, 2 * N], U8, name="w_words", align_bytes=64, offset=0)
        for w, src in enumerate((wa_words, wb_words, wo_words)):
            nc.sync.dma_start(w_words[:, w].bitcast(I32), src.rearrange("a p b -> p a b").bitcast(I32))
        state[0] = placed.tile([P, T], F32, name="state0", align_bytes=64, offset=7168)
        nc.sync.dma_start(state[0][:], r_rows[:, 0, :])

        def gather_words(dst, e, a, j0, j1):
            nc.vector.tensor_copy(dst, table[a][:].bitcast(U32).indirect(offsets(edge_lists[e], j0, j1)))

        first = keep.tile([P, 2, PASSES, HALF], U32, name="first", align_bytes=64)
        gather_words(first[:, 0, 0, :], 0, 0, 0, HALF)
        gather_words(first[:, 1, 0, :], 1, 0, 0, HALF)
        gather_words(first[:, 0, 1, :], 0, 1, 0, HALF)
        gather_words(first[:, 1, 1, :], 1, 1, 0, HALF)

        wc_codes = keep.tile([P, PASSES, N], U32, name="wc_codes", align_bytes=64)
        wc_planes = keep.tile([P, PASSES, N], U8, name="wc_planes", align_bytes=64)
        for a in range(PASSES):
            grouped = keep.tile([P, N, PACK], BF16, name="grouped%d" % (a,), tag="hold_a%d" % (a,), align_bytes=64)
            nc.scalar.copy(grouped[:], wc_raw[a][:].rearrange("p i n -> p n i"))
            nc.vector.quantize_mx(
                out=wc_codes[:, a, :].bitcast(FP8X4),
                scales=wc_planes[:, a, :],
                in_=grouped[:].rearrange("p n i -> p (n i)"),
            )

        load_state(1, "hold_a0", 64)
        load_state(2, "hold_a1", 64)
        second = []
        for a in range(PASSES):
            second.append(keep.tile([P, 2, HALF], U32, name="second%d" % (a,), tag="early%d" % (a,), align_bytes=64))
            for e in range(2):
                gather_words(second[a][:, e, :], e, a, HALF, J)
        load_state(3, "late1", 64)


        def picked(b, e, a):
            h, c = divmod(b * P, HALF)
            plane = (picked_planes, moved)[a][:, e, b * P : (b + 1) * P]
            words = first[:, e, a, c : c + P] if h == 0 else second[a][:, e, c : c + P]
            return words.bitcast(FP8X4), plane

        def dealing(tile):
            return tile[:].rearrange("j t m -> j m t")

        def by_word(bank):
            return bank[:].rearrange("j (m t) -> j m t", t=PACK)

        edge_weight = keep.tile([P, J // P], F32, name="edge_weight")
        bank = psum.tile([P, P], F32, name="turned")
        nc.tensor.transpose(bank[:], weight_rows[:], ident[:])
        nc.scalar.copy(edge_weight[:], bank[:, 0 : J // P])
        weight = keep.tile([P, J], F32, name="weight", align_bytes=64)
        for h in range(2):
            bank = psum.tile([P, 4, P], F32, name="turned")
            for s in range(4):
                b = 4 * h + s
                nc.tensor.transpose(bank[:, s, :], edge_weight[:, b : b + 1].to_broadcast([P, P]), ident[:])
            nc.scalar.copy(weight[:, h * HALF : (h + 1) * HALF], bank[:].rearrange("p s j -> p (s j)"))

        residual = [keep.tile([P, J], F32, name="residual%d" % (t,)) for t in range(3)]
        message = {}
        own = {}

        gate = {}

        def group(b, bank, terms):
            for i, (e, a, rhs, rhs_plane) in enumerate(terms):
                words, plane = picked(b, e, a)
                nc.tensor.matmul_mx(out=bank[:], lhsT=words, lhsT_scale=plane, rhs=rhs, rhs_scale=rhs_plane,
                                    start=(i == 0), stop=(i == len(terms) - 1))

        def fp4(w, a):
            return w_words[:, w, a, :].bitcast(FP4X4), w_planes[:, w, a, :]

        def packed_products(b):
            za = psum.tile([P, N], F32, name="za")
            group(b, za, [(e, a) + fp4(e, a) for a in range(PASSES) for e in range(2)])
            ow = psum.tile([P, N], F32, name="ow")
            group(b, ow, [(0, a) + fp4(2, a) for a in range(PASSES)])
            if b % 4 == 3:
                gate[b] = residual[2][:, (b // 4) * HALF : (b // 4 + 1) * HALF]
            else:
                gate[b] = keep.tile([P, N], F32, name="eta%d" % (b,))[:]
            nc.scalar.activation(gate[b].rearrange("j (t m) -> j m t", t=PACK), by_word(za), SIGMOID)
            if b == 7:
                own[b] = placed.tile([P, PACK, P], F32, name="own7", align_bytes=64, offset=18944)
            else:
                own[b] = keep.tile([P, PACK, P], F32, name="own%d" % (b,), tag="own%d" % (b,), align_bytes=64)
            nc.scalar.activation(dealing(own[b]), by_word(ow), COPY, scale=edge_weight[:, b : b + 1])

        def gated_message(b):
            ms = psum.tile([P, N], F32, name="ms")
            group(b, ms, [(1, a, wc_codes[:, a, :].bitcast(FP8X4), wc_planes[:, a, :]) for a in range(PASSES)])
            sent = keep.tile([P, PACK, P], F32, name="sent%d" % (b,))
            nc.scalar.activation(dealing(sent), by_word(ms), COPY, scale=edge_weight[:, b : b + 1])
            message[b] = keep.tile([P, PACK, P], F32, name="message%d" % (b,))
            nc.vector.tensor_tensor(message[b][:].rearrange("j t m -> j (t m)"), sent[:].rearrange("j t m -> j (t m)"), gate[b], MULT)

        def products(b):
            packed_products(b)
            gated_message(b)

        def turn(dst, parts, tag):
            bank = psum.tile([P, 4, P], F32, name="turned", tag=tag)
            for s, (t, b) in enumerate(parts):
                nc.tensor.matmul(bank[:, s, :], own[b][:, ORDER[t], :], ident[:], start=True, stop=False, is_transpose=True)
                nc.tensor.matmul(bank[:, s, :], message[b][:, ORDER[t], :], ident[:], start=False, stop=True, is_transpose=True)
            nc.scalar.copy(dst, bank[:].rearrange("p s j -> p (s j)"))

        def gather_state(t, j0, j1, out=None):
            out = residual[t][:, j0:j1] if out is None else out
            nc.vector.tensor_tensor(out, state[t][:].indirect(offsets(dst_list, j0, j1)), weight[:, j0:j1], MULT)

        summed = [keep.tile([P, J], F32, name="summed%d" % (t,)) for t in range(PACK)]

        def turn_half(t, h):
            turn(summed[t][:, h * HALF : (h + 1) * HALF], [(t, b) for b in range(4 * h, 4 * h + 4)], "turned" if t < 2 else "ms")

        def scatter(t, j0, j1, part=None):
            part = residual[t][:, j0:j1] if part is None else part
            nc.vector.tensor_tensor(pages[t % 2][:].indirect(offsets(dst_list, j0, j1)), part, summed[t][:, j0:j1], ADD)

        gather_state(0, 0, J)
        gather_state(1, 0, J)
        for h in range(2):
            j0, j1 = h * HALF, (h + 1) * HALF
            for b in range(5 * h, 4 * h + 4):
                products(b)
            gather_state(2, j0, j1)
            if h == 0:
                products(4)
            for t in range(2):
                turn_half(t, h)
                scatter(t, j0, j1)
        gather_state(3, 0, HALF, residual[0][:, HALF:J])
        for t in range(2, PACK):
            for h in range(2):
                turn_half(t, h)

        out_rows = out_0.rearrange("(p i) t -> p i t", i=PACK)
        woven = keep.tile([P, T, PACK], BF16, name="woven", tag="late0", align_bytes=64)
        parts = ((0, LEAD), (LEAD, SPLIT), (SPLIT, T))
        rounded = [
            placed.tile([P, 2, c1 - c0], BF16, name="rounded%d" % (k,), align_bytes=64, offset=(19456, 20480, 15872)[k])
            for k, (c0, c1) in enumerate(parts)
        ]
        for t in range(2):
            nc.sync.dma_start(out_rows[:, ORDER[t], :], pages[t][:])
            for k, (c0, c1) in enumerate(parts):
                if (t, k) != (1, 0):
                    nc.scalar.copy(rounded[k][:, t, :], pages[t][:, c0:c1])
                else:
                    nc.vector.tensor_copy(rounded[k][:, t, :], pages[t][:, c0:c1])
        for k, (c0, c1) in enumerate(parts):
            nc.scalar.copy(woven[:, c0:c1, 0:PACK:2], rounded[k][:].rearrange("p t c -> p c t"))
        scatter(2, 0, J)
        nc.sync.dma_start(out_rows[:, ORDER[2], :], pages[0][:])
        for c0, c1 in ((0, SPLIT), (SPLIT, T)):
            nc.scalar.copy(woven[:, c0:c1, 1], pages[0][:, c0:c1])
        last = placed.tile([P, HALF], F32, name="residual3", align_bytes=64, offset=19456)
        gather_state(3, HALF, J, last[:])
        scatter(3, 0, HALF, residual[0][:, HALF:J])
        scatter(3, HALF, J, last[:])
        nc.sync.dma_start(out_rows[:, ORDER[3], :], pages[1][:])
        for c0, c1 in ((0, CHUNK), (CHUNK, SPLIT)):
            nc.vector.tensor_copy(woven[:, c0:c1, 3], pages[1][:, c0:c1])
        for c0, c1 in ((SPLIT, T - CHUNK), (T - CHUNK, T)):
            nc.scalar.copy(woven[:, c0:c1, 3], pages[1][:, c0:c1])
        out_plane = keep.tile([P, T], U8, name="out_plane", align_bytes=64)
        out_words = out_1[0].rearrange("p t i -> p (t i)").bitcast(I32)
        for c in range(4):
            cols = slice(c * CHUNK, (c + 1) * CHUNK)
            codes = keep.tile([P, CHUNK], U32, name="codes%d" % (c,), align_bytes=64)
            nc.vector.quantize_mx(
                out=codes[:].bitcast(FP8X4),
                scales=out_plane[:, cols],
                in_=woven[:, cols, :].rearrange("p c i -> p (c i)"),
            )
            nc.sync.dma_start(out_words[:, cols], codes[:].bitcast(I32))
        for q in range(4):
            eng = nc.sync if q % 2 == 0 else nc.scalar
            eng.dma_start(out_2[0, 4 * q : 4 * q + 4, :].bitcast(I32), out_plane[32 * q : 32 * q + 4, :].bitcast(I32))
